import numpy as np, ml_dtypes
CORES = [9,25,41,57]
N = 4
BF = ml_dtypes.bfloat16
L, F, M, Q, S, R, C, P = 1024, 512, 1024, 4, 3, 2, 128, 4
A, ND, W = L + F, Q * M, L + F + Q * M
def pull(y, ix):
    return np.take_along_axis(y, ix[:, :, None, :], 3)
def evaluate(y, kd, om):
    for l in range(Q):
        i = l * M
        a = pull(y, kd[:, :, i:i + M]); b = pull(y, kd[:, :, ND + i:ND + i + M])
        y[..., A + i:A + i + M] = np.where(om[:, :, None, i:i + M] == 1, np.maximum(a, b), np.minimum(a + b, 255))
def begin(v, kd, om):
    y = np.zeros((N, 8, 16, W), np.int64); y[..., :A] = v
    evaluate(y, kd, om)
    return y
def values(rng, lo, hi):
    return (rng.random((N, 8, 16, A)) * np.exp2(rng.integers(lo, hi + 1, (N, 8, 1, A)))).astype(np.int64)
def kids(rng, near, other):
    k = np.zeros((N, 8, 2, Q, M), np.int64); sh = (N, 8, 2, M)
    for l in range(Q):
        c = rng.random(sh)
        x = rng.integers(A + max(l - 1, 0) * M, A + max(l, 1) * M, sh); z = rng.integers(0, A + l * M, sh); e = rng.integers(0, A, sh)
        k[:, :, :, l] = np.where((c < near) & (l > 0), x, np.where(c < near + other, z, e))
    return k
def aims(rng, v, k, o, share):
    y = begin(v, k.reshape(N, 8, 2 * ND), o)[..., W - M:]
    e = rng.random((N, 8, 1, M)); close = np.clip(y + rng.integers(-20, 21, y.shape), 0, 255)
    far = (rng.random(y.shape) * np.exp2(rng.integers(4, 9, (N, 8, 1, M)))).astype(np.int64)
    return np.where(e < share, y, np.where(e < share + (1 - share) * 0.5, close, far))
def ops(rng, share):
    return (rng.random((N, 8, ND)) < share).astype(np.int64)
def weights(rng, share):
    return (rng.random((N, 8, 16, 2)) < share).astype(np.int64)
def pack(v, k, o, g, w):
    return {"lv": np.ascontiguousarray(v.reshape(N, 128, A)).astype(np.float32).astype(BF), "kid": np.ascontiguousarray(k.reshape(N, 8, 2 * ND)).astype(np.int32),
            "mx": np.ascontiguousarray(o).astype(np.int32), "tg": np.ascontiguousarray(g.reshape(N, 128, M)).astype(np.float32).astype(BF),
            "wt": np.ascontiguousarray(w.reshape(N, 128, 2)).astype(np.int32)}
def setup_inputs(rng):
    v = values(rng, 4, 8); k = kids(rng, 0.5, 0.25); o = ops(rng, 0.4)
    return pack(v, k, o, aims(rng, v, k, o, rng.choice(np.array([0.2, 0.5, 0.8, 0.97]), (N, 8, 1, 1))), weights(rng, 0.6))
def setup_inputs_room(rng):
    v = rng.integers(1, 128, (N, 8, 16, A)); v[..., L:L + 2] = 0; v[:, :, 0, L + 1] = 1
    k = kids(rng, 0.5, 0.25); o = ops(rng, 0.4); w = weights(rng, 0.6)
    k[:, :, :, Q - 1] = rng.integers(0, A, (N, 8, 2, M)); o[:, :, ND - M:] = 0
    g = pull(v, k[:, :, 0, Q - 1]) + pull(v, k[:, :, 1, Q - 1])
    for q in range(N):
        for j in range(8):
            n = int(rng.choice(np.array([0, 1, C - 1, C, C + 1, M])))
            if q == 0: n = (C, C + 1, M, C - 1, 1, 0, C, C + 1)[j]
            at = np.arange(M - n, M) if q == 0 and j < 4 else rng.permutation(M)[:n]
            k[q, j, :, Q - 1, at] = L; g[q, j, :, at] = rng.integers(128, 256, (n, 16))
    k[0, 0:4:3, 1, Q - 1, M - 1] = L + 1; o[0, 0:4:3, ND - 1] = 1
    return pack(v, k, o, g, w)
def setup_inputs_ties(rng):
    few = np.array([0, 1, 2, 127, 128, 254, 255]); pal = rng.choice(few, (N, 8, 16, 6)).astype(np.int64)
    v = pull(pal, rng.integers(0, 6, (N, 8, A))); k = kids(rng, 0.4, 0.2)
    k[:, :, 1] = np.where(rng.random((N, 8, Q, M)) < 0.3, k[:, :, 0], k[:, :, 1])
    g = np.where(rng.random((N, 8, 1, M)) < 0.5, pull(pal, rng.integers(0, 6, (N, 8, M))), rng.choice(few, (N, 8, 16, M)))
    return pack(v, k, ops(rng, 0.5), g, weights(rng, 0.5))
def setup_inputs_meet(rng):
    v = values(rng, 3, 6); k = kids(rng, 0.5, 0.25)
    for l in range(1, Q):
        some = rng.integers(0, M, (N, 8, 8))
        k[:, :, :, l] = A + (l - 1) * M + np.take_along_axis(some, rng.integers(0, 8, (N, 8, 2 * M)), 2).reshape(N, 8, 2, M)
    k[:, 1::2, :, Q - 1] = k[:, 1::2, :, Q - 1, :1]
    return pack(v, k, ops(rng, 0.7), rng.integers(0, 256, (N, 8, 16, M)), weights(rng, 0.6))
def setup_inputs_ends(rng):
    v = np.where(rng.random((N, 8, 16, A)) < rng.random((N, 8, 1, A)), 255, 0)
    k = kids(rng, 1.0, 0.0); o = ops(rng, 0.5); w = weights(rng, 0.6); w[:, 0::4] = 1; w[:, 1::4] = 0
    for l in range(Q):
        c = [0, L - 1, L, A - 1] + ([A, A + (l - 1) * M, A + l * M - 1] if l else [])
        k[:, 0::2, :, l] = rng.choice(np.array(c), (N, 4, 2, M))
    g = np.where(rng.random((N, 8, 16, M)) < rng.random((N, 8, 1, M)), 255, 0)
    g[..., 0] = 255; g[..., M - 1] = 255; g[..., 1] = 0
    o[..., ND - M] = 1
    for j in (0, 4, 6):
        k[:, j, :, Q - 1, 0] = 0; v[:, j, :, 0] = 0; v[:, j, 0, 1:L] = 255
    w[:, 4] = 1; w[:, 4, 15, 0] = 0; g[:, 4, 15, 0] = 111
    w[:, 6] = 1; w[:, 6, 15, 0] = 0; v[:, 6, :, 1:L] = rng.integers(0, 5, (N, 16, L - 1)); v[:, 6, 0, 1:L] = rng.integers(1, 5, (N, L - 1))
    return pack(v, k, o, g, w)
def setup_inputs_spread(rng):
    v = (rng.random((N, 8, 16, A)) * np.exp2(8 * rng.random((N, 8, 1, A)))).astype(np.int64) * (rng.random((N, 8, 1, A)) > 0.0625)
    near = rng.random((N, 8, 1, 1)); k = kids(rng, near, (1 - near) * rng.random((N, 8, 1, 1))); o = ops(rng, rng.random((N, 8, 1)))
    return pack(v, k, o, aims(rng, v, k, o, rng.random((N, 8, 1, 1))), weights(rng, rng.random((N, 8, 1, 2))))
def check_inputs(d):
    bad = []
    for nm in ("lv", "tg"):
        x = d[nm].astype(np.float32)
        if not (np.min(x) >= 0 and np.max(x) <= 255): bad.append("range of " + nm)
        if np.any(x != np.floor(x)): bad.append("whole numbers in " + nm)
    for nm in ("mx", "wt"):
        if np.min(d[nm]) < 0 or np.max(d[nm]) > 1: bad.append("range of " + nm)
    k = d["kid"].reshape(N, 8, 2, Q, M)
    for l in range(Q):
        if np.min(k[:, :, :, l]) < 0 or np.max(k[:, :, :, l]) >= A + l * M: bad.append("range of kid in level " + str(l))
    return bad
def reference(lv, kid, mx, tg, wt):
    kd = kid.astype(np.int64); om = mx.astype(np.int64)
    y = begin(lv.astype(np.float32).astype(np.int64).reshape(N, 8, 16, A), kd, om)
    goal = tg.astype(np.float32).astype(np.int64).reshape(N, 8, 16, M); w = wt.astype(np.int64).reshape(N, 8, 16, 2)
    for rnd in range(R):
        node = np.tile(ND - M + np.arange(M), (N, 8, 1)); live = np.ones((N, 8, M), bool); want = goal
        par = np.zeros((N, 8, M), np.int64); side = np.zeros((N, 8, M), np.int64); child = np.zeros((N, 8, M), np.int64); err = np.zeros((N, 8, M), np.int64)
        for step in range(S):
            ka = np.take_along_axis(kd, node, 2); kb = np.take_along_axis(kd, node + ND, 2); o = np.take_along_axis(om, node, 2)[:, :, None, :] == 1
            ya = pull(y, ka); yb = pull(y, kb)
            wa = np.where(o, np.where(want >= yb, want, 0), np.maximum(want - yb, 0))
            wb = np.where(o, np.where(want >= ya, want, 0), np.maximum(want - ya, 0))
            ea = np.add.reduce(np.abs(wa - ya), axis=2); eb = np.add.reduce(np.abs(wb - yb), axis=2)
            tob = eb < ea
            par = np.where(live, node, par); side = np.where(live, tob, side); child = np.where(live, np.where(tob, kb, ka), child); err = np.where(live, np.where(tob, eb, ea), err)
            want = np.where(live[:, :, None, :], np.where(tob[:, :, None, :], wb, wa), want)
            live = live & (child >= A); node = np.where(live, child - A, 0)
        u1 = np.add.reduce(w[..., 0:1] * want, axis=2); u2 = np.add.reduce(w[..., 1:2] * want, axis=2)
        h = ((u1 * u2) >> 5) + u2; stride = 2 * (u1 & 127) + 1
        cand = (h[:, :, None, :] + np.arange(P)[None, None, :, None] * stride[:, :, None, :]) & (L - 1)
        off = np.abs(pull(y, cand.reshape(N, 8, P * M)).reshape(N, 8, 16, P, M) - want[:, :, :, None, :])
        ce = np.add.reduce(off, axis=2); m = np.argmin(ce, axis=2)
        donor = np.take_along_axis(cand, m[:, :, None, :], 2)[:, :, 0]
        hit = np.min(ce, axis=2) < err; one = hit.astype(np.int64)
        counts = hit & (np.add.accumulate(one, axis=2) - one < C)
        go = {}
        for q in range(N):
            for g in range(8):
                i = np.flatnonzero(counts[q, g]); go[q, g] = y[q, g][:, child[q, g, i]]
                key, first = np.unique(side[q, g, i] * ND + par[q, g, i], return_index=True)
                kd[q, g, key] = donor[q, g, i[first]]
        for q in range(N):
            for g in range(8):
                v = go[q, g]; y[(q + 1) % N, g, :, rnd * C:rnd * C + v.shape[1]] = v
        evaluate(y, kd, om)
    return {"yo": y.reshape(N, 128, W).astype(np.float32).astype(BF), "ko": kd.astype(np.float32)}

@@ -1,0 +1,711 @@
+from concourse.mybir import AluOpType, ActivationFunctionType, AxisListType
+
+ALU = AluOpType
+ACT = ActivationFunctionType
+X = AxisListType.X
+FX, GC, PC = 15.0, 1.3, 0.42
+HB0 = 2000.0
+CH = ((0, 256, "V"), (256, 256, "A"), (512, 256, "V"), (768, 256, "V"))
+L, A0, ND, W = 1024, 1536, 4096, 5632
+BIG = 1 << 20
+
+SCRATCH, META, PLACE = {}, {}, {}
+PACK = {"float32": "PKF", "bfloat16": "PKB", "int32": "PKI", "uint16": "PKU"}
+
+
+def _bufs(text, dt="float32", where="sbuf", rows=128):
+    for w in text.split():
+        name, cols = w.split(":")
+        META[name] = (where, [rows, int(cols)], dt)
+        if where == "sbuf" and rows == 128 and int(cols) <= 128 and name not in ("SEND", "RECV0", "RECV1", "WTI"):
+            off = SCRATCH.get(PACK[dt], (0, (0, 0)))[1][1]
+            PLACE[name] = (PACK[dt], off)
+            SCRATCH[PACK[dt]] = ("sbuf", [128, off + (int(cols) + 15) // 16 * 16], dt)
+        else:
+            SCRATCH[name] = META[name]
+
+
+def _halves(text):
+    return " ".join(n.replace(":", h + ":") for h in "01" for n in text.split())
+
+
+_bufs("U:5632 AT:4096 BT:4096 INFO:4224 SALL:2048 WA:2048 WB:2048 C1:2048 C2:2048 WBA:2048 N5B:128 P5B:128 IDB:128 NIB:128 BLK:128 LTI:128 "
+      "T4:128 LV:1536 TG:1024 TGC:1024 KH:512 KLO:512 YO:5632 YT:4096 WTB:2 HB:64 INVF:128 SEND:128 RECV0:128 RECV1:128 RG:128 RT:128 "
+      "DV1:128 DV2:128 DV:128 DVA:128 DVB:128 EQ:1024 OLDA:128 OLDB:128", "bfloat16")
+_bufs(_halves("WDA:1536 WDB:1536 T1:1024 ZS:1024 AB:1024 NF:512 XC:2048 AC:2048"), "bfloat16")
+_bufs(_halves("EB:32 TO:64 KAQ:64 KD:96 R:64 NDF:32 LIV:64 LQ:32 KE:64 KN:64 KDT:32 TK:32 CHD:32 CS:128 CK:128 CM:64 BST:32"))
+_bufs(_halves("UI:64 PR:32 SH:32 UA:32 STR:32 CI:128 CA:128 DI:32 DJ:32"), "int32")
+_bufs(_halves("NLA:64 NLB:64 NLC:64 CL:128"), "uint16")
+_bufs("IDF:128 BLKF:128 PF:1 PM:1 PG:1 EI:16 RA:1 RB:1 RBA:1 JQ2:32 MSK:128 RM:128 RD:128 R16:128 R8:8 SEG:128 ONE:64 KR1:128 KR0:128 KC:8 "
+      "DUM:8 JQ:64 JC:64 JT:64 MQ:128 K3F:128 WTF:2 K12:2 FM:4 NFM:2 CIN:64 RN:64 GT:192 SG:8 SGT:8 JNK:128 GV:384 SEL:384 MC:128 MS:128 "
+      "KX:128 IVB:128 KM:128 KMS:128 BI:16 SD:16 KEYW:8 ND1:8 LAB:16 OF:16 KO:512")
+_bufs("XK:512 XL:512 XH:512 WTI:2 PI:1 PJ:1 PK:1 KI:128 KEYI:128 DLO:128 DHI:128", "int32")
+_bufs("MXI:512 PI8:1 PJ8:1 PK8:1 KX0:256", "int32", rows=64)
+_bufs("NM:512 NMN:512 TE:1024 B8:128", "bfloat16", rows=64)
+_bufs("PQ8:1 PR8:1 E8:8 KXF:256", rows=64)
+_bufs("KL:512 CLST:24 CHL:8 OFU:16", "uint16")
+_bufs("DH:8192 DL:8192 DN:4096", "bfloat16", "dram", 8)
+_bufs("QH0:1024 QH1:1024 SM0:512 SM1:512 ZZ:1024", "float32", "psum")
+
+SEMAPHORES = ["sV", "sA", "sT", "sG", "rs0", "rs1", "ls0", "ls1"] + ["d%d" % i for i in range(60)]
+
+
+def V(name, a=None, b=None, s=1, p=None):
+    if a is None:
+        a, b = 0, META[name][1][1]
+    return (name, a, b, s, p)
+
+
+def IND(win, off):
+    return ("@", win, off)
+
+
+def _ap(T, v):
+    if isinstance(v, (int, float)):
+        return v
+    if v[0] == "@":
+        return _ap(T, v[1]).indirect(_ap(T, v[2]))
+    name, a, b, s, p = v
+    name, off = PLACE.get(name, (name, 0))
+    a, b, t = a + off, b + off, T[name]
+    if p is None:
+        return t[:, a:b] if s == 1 else t[:, a:b:s]
+    if p[2] == 1:
+        return t[p[0]:p[1], a:b] if s == 1 else t[p[0]:p[1], a:b:s]
+    return t[p[0]:p[1]:p[2], a:b]
+
+
+def _n(v):
+    if v[0] == "@":
+        return 16 * _n(v[2])
+    return len(range(v[1], v[2], v[3]))
+
+
+def _two(*vs):
+    for v in vs:
+        nm = v[1][0] if v[0] == "@" else v[0]
+        if META[nm][2] not in ("bfloat16", "uint16"):
+            return False
+    return True
+
+
+def _regs(vs):
+    out = []
+    for v in vs:
+        if isinstance(v, (int, float)) or v is None:
+            continue
+        if v[0] == "@":
+            out += [v[1], v[2]]
+        else:
+            out.append(v)
+    return out
+
+
+def build():
+    ops = []
+    bias = [0.0]
+
+    def op(eng, emit, rd, wr, cost, kind="c", info=None):
+        ops.append({"e": eng, "f": emit, "rd": _regs(rd) + [w[2] for w in wr if w[0] == "@"], "wr": [w[1] if w[0] == "@" else w for w in wr],
+                    "c": cost, "k": kind, "i": info, "b": bias[0]})
+
+    def vcost(out, a):
+        n = _n(out)
+        return 50 + GC * n if a[0] == "@" else FX + max((0.42 if _two(out, a) else 0.83) * n, 53)
+
+    def tt(out, a, b, alu):
+        n = _n(out)
+        if out[0] == "@":
+            c = 50 + 3.2 * n
+        elif a[0] == "@":
+            c = 50 + GC * n
+        else:
+            ps = META[a[0]][0] == "psum" or META[b[0]][0] == "psum"
+            c = FX + max((0.83 if ps else 1.66) * n, 53)
+        op("V", lambda g, T: g.vector.tensor_tensor(_ap(T, out), _ap(T, a), _ap(T, b), alu), [a, b], [out], c)
+
+    def ts(out, a, s1, o0, s2=None, o1=None):
+        if o1 is None:
+            op("V", lambda g, T: g.vector.tensor_scalar(_ap(T, out), _ap(T, a), _ap(T, s1), None, o0), [a, s1], [out], vcost(out, a))
+        else:
+            op("V", lambda g, T: g.vector.tensor_scalar(_ap(T, out), _ap(T, a), _ap(T, s1), _ap(T, s2), o0, o1), [a, s1, s2], [out], vcost(out, a))
+
+    def cp(out, a):
+        op("V", lambda g, T: g.vector.tensor_copy(_ap(T, out), _ap(T, a)), [a], [out], vcost(out, a))
+
+    def act(out, a, func, bias=0.0, scale=1.0, acc=None):
+        n = _n(out)
+        c = 65 + GC * n if a[0] == "@" else FX + 10 + 0.83 * max(n, 64)
+        wr = [out] + ([acc] if acc is not None else [])
+
+        def em(g, T):
+            k = {}
+            if not (isinstance(bias, float) and bias == 0.0):
+                k["bias"] = _ap(T, bias)
+            if not (isinstance(scale, float) and scale == 1.0):
+                k["scale"] = _ap(T, scale)
+            if acc is not None:
+                k["accum_out"] = _ap(T, acc)
+            return g.scalar.activation(_ap(T, out), _ap(T, a), func, **k)
+        op("A", em, [a, bias, scale], wr, c)
+
+    def scan(out, d0, d1):
+        op("V", lambda g, T: g.vector.tensor_tensor_scan(_ap(T, out), _ap(T, d0), _ap(T, d1), 0.0, ALU.mult, ALU.add), [d0, d1], [out], FX + 0.83 * _n(out))
+
+    def rsum(out, a):
+        op("V", lambda g, T: g.vector.tensor_reduce(_ap(T, out), _ap(T, a), X, ALU.add), [a], [out], FX + max(0.83 * _n(a), 53))
+
+    def memset(out, c):
+        op("V", lambda g, T: g.vector.memset(_ap(T, out), c), [], [out], FX + 0.42 * _n(out))
+
+    def iota(out, pattern, base, cm, flag=True):
+        if flag:
+            op("G", lambda g, T: g.iota(_ap(T, out), pattern, base, cm, allow_small_or_imprecise_dtypes=True), [], [out], 130 + 1.66 * _n(out))
+        else:
+            op("G", lambda g, T: g.iota(_ap(T, out), pattern, base, cm), [], [out], 130 + 1.66 * _n(out))
+
+    def mms(lst, start=True, stop=True, f32=False):
+        c = 40.0
+        for o, w, r in lst:
+            c += PC * max(64, _n(r)) * (4 if f32 else 1)
+
+        def em(g, T):
+            last = None
+            for q, (o, w, r) in enumerate(lst):
+                last = g.tensor.matmul(_ap(T, o), _ap(T, w), _ap(T, r), start and q == 0, stop and q == len(lst) - 1)
+            return last
+        op("T", em, [w for o, w, r in lst] + [r for o, w, r in lst] + ([] if start else [lst[0][0]]), [lst[0][0]], c)
+
+    def tp(out, a, ident):
+        op("T", lambda g, T: g.tensor.transpose(_ap(T, out), _ap(T, a), _ap(T, ident)), [a, ident], [out], 200)
+
+    def dma(q, out, a, c=2000):
+        def em(g, T):
+            return {"S": g.sync, "A": g.scalar}[q].dma_start(_ap(T, out), _ap(T, a))
+        op(q, em, [a] if a[0] in META else [], [out] if out[0] in META else [], c, "d")
+
+    def wrap(out, mats, src, a, b):
+        mms([(out, V(mats, 128 * i, 128 * i + 128), V(src, a + i, b, 16)) for i in range(16)])
+
+    dma("S", V("LV"), ("lv", 0, A0, 1, None), 2500)
+    for gq in range(8):
+        for sd in range(2):
+            dma("S" if gq < 4 else "A", V("KX0", sd * 128 + gq * 16, sd * 128 + gq * 16 + 16), ("kid", sd * ND, sd * ND + 1024, 1, (gq, gq + 1, 1)), 2500)
+    dma("A", V("MXI"), ("mx", 0, ND, 1, None))
+    dma("S", V("XK"), ("kid", 0, 8192, 1, None))
+    dma("S", V("TG"), ("tg", 0, 1024, 1, None))
+    dma("S", V("WTI"), ("wt", 0, 2, 1, None))
+    bias[0] = 20000.0
+    iota(V("PI"), [[0, 1]], 0, 1, False)
+    iota(V("RM"), [[1, 128]], 0, 0)
+    iota(V("RD"), [[1, 8], [0, 16]], 0, 0)
+    iota(V("PI8"), [[0, 1]], 0, 1, False)
+    iota(V("R16"), [[0, 8], [1, 16]], 0, 0)
+    iota(V("R8"), [[1, 8]], 0, 0)
+    cp(V("PF"), V("PI"))
+    ts(V("IDF"), V("RM"), V("PF"), ALU.is_equal)
+    cp(V("KXF"), V("KX0"))
+    act(V("U", 0, A0), V("LV"), ACT.Identity, 255.0, -1.0)
+    p64 = (0, 64, 1)
+    for sd in range(2):
+        tp(V("SM0", 64 * sd, 64 * sd + 64), V("KXF", 128 * sd, 128 * sd + 128), V("IDF", 0, 64, 1, p64))
+    cp(V("KL", 0, 128), V("SM0", 0, 128))
+    bias[0] = 6000.0
+    ts(V("PJ"), V("PI"), 15, ALU.bitwise_and)
+    cp(V("PM"), V("PJ"))
+    ts(V("PK"), V("PI"), 4, ALU.arith_shift_right)
+    cp(V("PG"), V("PK"))
+    ts(V("BLK"), V("RD"), V("PG"), ALU.is_equal)
+    ts(V("EI"), V("R16", 0, 16), V("PM"), ALU.is_equal)
+    ts(V("RA"), V("EI", 0, 1), 256.0, ALU.mult, V("EI", 1, 2), ALU.add)
+    ts(V("RB"), V("EI", 2, 3), 256.0, ALU.mult, V("EI", 3, 4), ALU.add)
+    cp(V("IDB"), V("IDF"))
+    ts(V("PJ8"), V("PI8"), 7, ALU.bitwise_and)
+    cp(V("PR8"), V("PJ8"))
+    ts(V("PK8"), V("PI8"), 3, ALU.arith_shift_right)
+    cp(V("PQ8"), V("PK8"))
+    ts(V("B8"), V("RD", 0, 128, 1, p64), V("PQ8"), ALU.is_equal)
+    ts(V("E8"), V("R8", 0, 8, 1, p64), V("PR8"), ALU.is_equal)
+    for q in range(8):
+        act(V("TE", 128 * q, 128 * q + 128), V("B8"), ACT.Copy, 0.0, V("E8", q, q + 1))
+    bias[0] = 3000.0
+    memset(V("SALL"), 0.0)
+    for i in range(16):
+        act(V("SALL", 129 * i, 129 * i + 113, 16), V("BLK", i, 128, 16), ACT.Copy)
+    bias[0] = 6000.0
+    memset(V("INFO"), 0.0)
+    ts(V("NM"), V("MXI"), -255.0, ALU.mult, 255.0, ALU.add)
+    act(V("NMN"), V("NM"), ACT.Copy, 0.0, -1.0)
+    ts(V("XH"), V("XK"), 8, ALU.arith_shift_right)
+    ts(V("XL"), V("XK"), 255, ALU.bitwise_and)
+    ts(V("KH"), V("XH"), -6.0, ALU.add)
+    cp(V("KLO"), V("XL"))
+    dma("S", V("DH"), V("KH"))
+    dma("S", V("DL"), V("KLO"))
+    dma("S", V("DN"), V("NM"))
+    for f, (d, a) in enumerate((("DH", 0), ("DL", 0), ("DH", ND), ("DL", ND), ("DN", 0))):
+        dma("S", V("INFO", 0, ND, 1, (f, 128, 16)), V(d, a, a + ND))
+    bias[0] = 2000.0
+    ts(V("WA"), V("SALL"), V("RA"), ALU.mult)
+    ts(V("WB"), V("SALL"), V("RB"), ALU.mult)
+    bias[0] = 0.0
+
+    def relist(l):
+        P = ("SM0", "SM1")[l & 1]
+        wrap(V(P, 0, 64), "WA", "INFO", 1024 * l, 1024 * l + 1024)
+        wrap(V(P, 64, 128), "WB", "INFO", 1024 * l, 1024 * l + 1024)
+        ts(V("KL", 128 * l, 128 * l + 128), V(P, 0, 128), float(A0), ALU.add)
+        if l == 3:
+            act(V("K3F"), V(P, 0, 128), ACT.Copy)
+
+    def outputs(l):
+        if l == 0:
+            ts(V("YO", 0, A0), V("U", 0, A0), -1.0, ALU.mult, 255.0, ALU.add)
+            dma("S", ("yo", 0, A0, 1, None), V("YO", 0, A0))
+        for c0 in (1024 * l, 1024 * l + 512):
+            u, yt, yo = V("U", A0 + c0, A0 + c0 + 512), V("YT", c0, c0 + 512), V("YO", A0 + c0, A0 + c0 + 512)
+            if l < 3:
+                act(yt, u, ACT.Relu)
+                act(yo, yt, ACT.Identity, 255.0, -1.0)
+            else:
+                ts(yt, u, -1.0, ALU.mult, 0.0, ALU.min)
+                ts(yo, yt, 255.0, ALU.add)
+            dma("S", ("yo", A0 + c0, A0 + c0 + 512, 1, None), yo)
+        if l == 0:
+            lst = []
+            for q in range(8):
+                rhs = V("INFO", 512 * q, 512 * q + 512)
+                lst.append((V("ZZ", 0, 512), V("WA", 128 * q, 128 * q + 128), rhs))
+                lst.append((V("ZZ", 0, 512), V("WB", 128 * (8 + q), 128 * (8 + q) + 128), rhs))
+            for q in range(0, 16, 2):
+                mms(lst[q:q + 2], q == 0, q == 14)
+            act(V("KO"), V("ZZ", 0, 512), ACT.Identity, float(A0))
+            dma("S", ("ko", 0, 8192, 1, None), V("KO"))
+
+    def evaluate(first, final):
+        if not first:
+            relist(0)
+        for l in range(4):
+            base = 1024 * l
+            win = V("U", 0, A0 + base)
+            pss = []
+            for q, (c0, w, eb) in enumerate(CH):
+                ps = V("QH%d" % (q // 2), 512 * (q % 2), 512 * (q % 2) + w)
+                pss.append(ps)
+                k0 = 2 * l + c0 // 512
+                mms([(ps, V("TE", 128 * k0, 128 * k0 + 128), V("NMN", c0 % 512, c0 % 512 + w))], True, False)
+            for q, (c0, w, eb) in enumerate(CH):
+                c, k0 = base + c0, 128 * l + c0 // 16
+                act(V("AT", c, c + w), IND(win, V("KL", k0, k0 + w // 16)), ACT.Relu)
+                off = V("KL", k0 + 64, k0 + 64 + w // 16)
+                if eb == "A":
+                    act(V("BT", c, c + w), IND(win, off), ACT.Relu)
+                else:
+                    ts(V("BT", c, c + w), IND(win, off), 0.0, ALU.max)
+            for q, (c0, w, eb) in enumerate(CH):
+                c, ps = base + c0, pss[q]
+                mms([(ps, V("IDB"), V("AT", c, c + w)), (ps, V("IDB"), V("BT", c, c + w))], False, True)
+                tt(ps, ps, V("AT", c, c + w), ALU.min)
+                tt(V("U", A0 + c, A0 + c + w), ps, V("BT", c, c + w), ALU.min)
+            if l < 3:
+                relist(l + 1)
+            if final:
+                outputs(l)
+
+    evaluate(True, False)
+
+    ts(V("NIB"), V("IDB"), -1.0, ALU.mult)
+    ts(V("N5B"), V("IDB"), -512.0, ALU.mult)
+    ts(V("P5B"), V("IDB"), 512.0, ALU.mult)
+    ts(V("TGC"), V("TG"), -1.0, ALU.mult, 255.0, ALU.add)
+    ts(V("T4"), V("BLK"), V("EI", 4, 5), ALU.mult)
+    iota(V("JC"), [[16, 64]], 0, 0)
+    iota(V("KR1"), [[1, 128]], 1, 0)
+    iota(V("MQ"), [[1024, 4], [0, 32]], 0, 0)
+    iota(V("DUM"), [[16, 8]], 0, 0)
+    ts(V("JQ"), V("JC"), V("PM"), ALU.add)
+    ts(V("JT"), V("JQ"), 3072.0, ALU.add)
+    ts(V("JQ2"), V("JQ", 0, 32), 1024.0, ALU.add)
+    cp(V("WTB"), V("WTI"))
+    cp(V("WTF"), V("WTI"))
+    act(V("C1"), V("SALL"), ACT.Copy, 0.0, V("WTF", 0, 1))
+    act(V("C2"), V("SALL"), ACT.Copy, 0.0, V("WTF", 1, 2))
+    tt(V("RBA"), V("RB"), V("RA"), ALU.subtract)
+    act(V("WBA"), V("SALL"), ACT.Copy, 0.0, V("RBA"))
+    mms([(V("SM0", 0, 2), V("BLK"), V("WTB"))])
+    ts(V("K12"), V("SM0", 0, 2), 255.0, ALU.mult)
+    ts(V("LTI"), V("RM"), V("PF"), ALU.is_ge)
+    tt(V("LTI"), V("LTI"), V("BLK"), ALU.mult)
+    cp(V("BLKF"), V("BLK"))
+    ts(V("MSK"), V("R16"), V("PM"), ALU.is_equal)
+    ts(V("SEG"), V("R16"), 0.0, ALU.is_gt)
+    memset(V("ONE"), 1.0)
+    ts(V("KR0"), V("RM"), 1.0, ALU.mult)
+    ts(V("KC"), V("DUM"), V("PM"), ALU.add, 0.5, ALU.add)
+    ts(V("DUM"), V("KC"), ND - 0.5, ALU.add)
+    tt(V("FM", 0, 1), V("EI", 0, 1), V("EI", 2, 3), ALU.add)
+    tt(V("FM", 1, 2), V("EI", 1, 2), V("EI", 3, 4), ALU.add)
+    tt(V("FM", 2, 3), V("EI", 0, 1), V("EI", 1, 2), ALU.add)
+    tt(V("FM", 3, 4), V("EI", 2, 3), V("EI", 3, 4), ALU.add)
+    ts(V("NFM"), V("FM", 2, 4), -1.0, ALU.mult, 1.0, ALU.add)
+
+    def down():
+        for s in range(3):
+            for h in range(2):
+                H = str(h)
+                bias[0] = HB0 * (1 - h)
+                cur, nxt = (("WDA", "WDB") if s % 2 == 0 else ("WDB", "WDA"))
+                cur, nxt = cur + H, nxt + H
+                NLn, NLp = ("NLA", "NLB", "NLC")[s] + H, ("NLA", "NLB", "NLC")[s - 1] + H
+                Q, SM, ZS, AB, NF, T1 = "QH" + H, "SM" + H, "ZS" + H, "AB" + H, "NF" + H, "T1" + H
+                R, TO, KAQ, KD, EB, KE, KN, LIV = "R" + H, "TO" + H, "KAQ" + H, "KD" + H, "EB" + H, "KE" + H, "KN" + H, "LIV" + H
+                jq = V("JQ", 0, 32)
+                bank = (V(SM), V(Q, 512, 1024))
+                if s == 0:
+                    D = V("TGC", 512 * h, 512 * h + 512)
+                    own = (V("AT", 3072 + 512 * h, 3584 + 512 * h), V("BT", 3072 + 512 * h, 3584 + 512 * h))
+                    ka, kb = V("K3F", 32 * h, 32 * h + 32), V("K3F", 64 + 32 * h, 96 + 32 * h)
+                    act(V(KAQ, 0, 32), ka, ACT.Copy)
+                    act(V(KAQ, 32, 64), jq, ACT.Copy)
+                    tt(V(KD, 32, 64), kb, ka, ALU.subtract)
+                    act(V(KD, 64, 96), jq, ACT.Identity, 512.0, 0.0)
+                    zs = [[(1, own[1 - x]), (-1, D)] for x in range(2)]
+                    nm = (V("TE", 128 * (6 + h), 128 * (7 + h)), V("NM"))
+                else:
+                    D = V(cur, 1024, 1536)
+                    act(D, IND(V(nxt, 0, 1024 if s == 1 else 1536), V(NLp, 32, 64)), ACT.Copy)
+                    nl = V(NLp, 0, 32)
+                    za, yb = V(ZS, 0, 512), V(ZS, 512, 1024)
+                    act(yb, IND(V("BT", 0, 3072), nl), ACT.Copy)
+                    tt(za, IND(V("AT", 0, 3072), nl), D, ALU.subtract)
+                    act(V(NF), IND(V("INFO", 0, ND), nl), ACT.Copy)
+                    zs = [[(1, yb), (-1, D)], [(1, za)]]
+                    nm = (V("T4"), V(NF))
+                for x in range(2):
+                    q = V(Q, 512 * x, 512 * x + 512)
+                    mms([(q, V("N5B") if w > 0 else V("P5B"), r) for w, r in zs[x]])
+                    tt(V(T1, 512 * x, 512 * x + 512), q, D, ALU.max)
+                for x in range(2):
+                    mms([(bank[x],) + nm] + [(bank[x], V("NIB") if w > 0 else V("IDB"), r) for w, r in zs[x]])
+                if s > 0:
+                    z = 512 * h
+                    wrap(V("ZZ", z, z + 32), "WA", NF, 0, 512)
+                    wrap(V("ZZ", z + 32, z + 64), "WBA", NF, 0, 512)
+                    ch = V(R, 0, 32)
+                    act(V("NDF" + H), ch, ACT.Relu)
+                    ts(V(LIV, 0, 32), ch, 0.0, ALU.is_ge)
+                    act(V(LIV, 32, 64), V(LIV, 0, 32), ACT.Copy)
+                    act(V(KD, 64, 96), V(LIV, 0, 32), ACT.Copy, 0.0, 512.0)
+                    act(V("LQ" + H), V(LIV, 0, 32), ACT.Copy, 0.0, 1024.0)
+                    ts(V("CHD" + H), ch, 0.0, ALU.min)
+                    tt(V(KAQ, 32, 64), V("JQ2"), V("LQ" + H), ALU.subtract)
+                    tt(V(KD, 0, 64), V("ZZ", z, z + 64), V(LIV), ALU.mult)
+                    tt(V(KAQ, 0, 32), V(KD, 0, 32), V("CHD" + H), ALU.add)
+                for x in range(2):
+                    w = V(cur, 512 * x, 512 * x + 512)
+                    tt(w, bank[x], V(T1, 512 * x, 512 * x + 512), ALU.max)
+                    ts(w, w, 255.0, ALU.min)
+                for x in range(2):
+                    q = V(Q, 512 * x, 512 * x + 512)
+                    if s == 0:
+                        mine = [own[x]]
+                    else:
+                        mine = ([za, D], [yb])[x]
+                    mms([(q, V("IDB"), y) for y in mine] + [(q, V("NIB"), V(cur, 512 * x, 512 * x + 512))])
+                    act(V(AB, 512 * x, 512 * x + 512), q, ACT.Abs)
+                wrap(V(SM, 0, 64), "SALL", AB, 0, 1024)
+                act(V(EB), V(SM, 32, 64), ACT.Copy)
+                tt(V(TO, 0, 32), V(SM, 0, 32), V(EB), ALU.is_gt)
+                tt(V(TO, 32, 64), V(SM, 0, 32), V(EB), ALU.is_gt)
+                tt(V(KE, 32, 64) if s == 0 else V(KN, 32, 64), V(SM, 0, 32), V(EB), ALU.min)
+                tt(V(R), V(TO), V(KD, 32, 96), ALU.mult)
+                tt(V(R), V(R), V(KAQ), ALU.add)
+                ts(V(NLn), V(R), 0.0, ALU.max)
+                act(V("TK" + H), V(TO, 0, 32), ACT.Copy, 0.0, float(ND))
+                if s == 0:
+                    tt(V(KE, 0, 32), V("TK" + H), V("JT", 32 * h, 32 * h + 32), ALU.add)
+                else:
+                    tt(V(KN, 0, 32), V("TK" + H), V("NDF" + H), ALU.add)
+                    tt(V(KN), V(KN), V(KE), ALU.subtract)
+                    tt(V(KN), V(KN), V(LIV), ALU.mult)
+                    tt(V(KE), V(KE), V(KN), ALU.add)
+
+    def donors():
+        for h in range(2):
+            H = str(h)
+            bias[0] = HB0 * (1 - h)
+            D = V("WDB" + H, 1024, 1536)
+            act(D, IND(V("WDA" + H), V("NLC" + H, 32, 64)), ACT.Copy)
+            z = 512 * h
+            wrap(V("ZZ", z, z + 32), "C1", "WDB" + H, 1024, 1536)
+            wrap(V("ZZ", z + 32, z + 64), "C2", "WDB" + H, 1024, 1536)
+            UI, CI, CA, CL, CS, CK, CM, BST = "UI" + H, "CI" + H, "CA" + H, "CL" + H, "CS" + H, "CK" + H, "CM" + H, "BST" + H
+            for x in range(2):
+                ts(V(UI, 32 * x, 32 * x + 32), V("ZZ", z + 32 * x, z + 32 * x + 32), -1.0, ALU.mult, V("K12", x, x + 1), ALU.add)
+            tt(V("PR" + H), V(UI, 0, 32), V(UI, 32, 64), ALU.mult)
+            ts(V("SH" + H), V("PR" + H), 5, ALU.arith_shift_right)
+            ts(V("UA" + H), V(UI, 0, 32), 127, ALU.bitwise_and)
+            ts(V("STR" + H), V("UA" + H), 2.0, ALU.mult, 1.0, ALU.add)
+            tt(V(CI, 0, 32), V("SH" + H), V(UI, 32, 64), ALU.add)
+            for m in range(1, 4):
+                tt(V(CI, 32 * m, 32 * m + 32), V(CI, 32 * m - 32, 32 * m), V("STR" + H), ALU.add)
+            ts(V(CA), V(CI), 1023, ALU.bitwise_and)
+            cp(V(CL), V(CA))
+            for m in range(4):
+                x = V("XC" + H, 512 * m, 512 * m + 512)
+                win = IND(V("U", 0, L), V(CL, 32 * m, 32 * m + 32))
+                if m < 3:
+                    tt(x, win, D, ALU.subtract)
+                else:
+                    act(x, win, ACT.Copy)
+                    q = V("QH" + H, 0, 512)
+                    mms([(q, V("IDB"), x), (q, V("NIB"), D)])
+                    x = q
+                act(V("AC" + H, 512 * m, 512 * m + 512), x, ACT.Abs)
+            tt(V(CS), V(CA), V("MQ"), ALU.add)
+            ts(V(CS), V(CS), 1.0 / 4096, ALU.mult)
+            wrap(V("SM" + H, 0, 128), "SALL", "AC" + H, 0, 2048)
+            tt(V(CK), V("SM" + H, 0, 128), V(CS), ALU.add)
+            tt(V(CM), V(CK, 0, 64), V(CK, 64, 128), ALU.min)
+            tt(V(BST), V(CM, 0, 32), V(CM, 32, 64), ALU.min)
+            tt(V("HB", 32 * h, 32 * h + 32), V(BST), V("KE" + H, 32, 64), ALU.is_lt)
+            ts(V("DI" + H), V(BST), 4096.0, ALU.mult)
+            ts(V("DJ" + H), V("DI" + H), 1023, ALU.bitwise_and)
+            c = 64 + 32 * h
+            act(V("GT", c, c + 32), V("R" + H, 0, 32), ACT.Identity, float(A0))
+            ts(V("KDT" + H), V("KE" + H, 0, 32), 1024.0, ALU.mult)
+            tt(V("GT", c + 64, c + 96), V("KDT" + H), V("DJ" + H), ALU.add)
+
+    def count_send(t):
+        bias[0] = 0.0
+        mms([(V("QH0", 0, 64), V("BLK"), V("HB"))])
+        mms([(V("QH0", 64, 128), V("LTI"), V("HB"))])
+        scan(V("CIN"), V("ONE"), V("QH0", 0, 64))
+        for kc in range(8):
+            if kc < 4:
+                act(V("JNK", 0, 64), V("CIN"), ACT.Sign, V("KC", kc, kc + 1), -1.0, V("SG", kc, kc + 1))
+            else:
+                e = V("EQ", 64 * kc, 64 * kc + 64)
+                ts(e, V("CIN"), V("KC", kc, kc + 1), ALU.is_lt)
+                rsum(V("SGT", kc, kc + 1), e)
+        tt(V("RN"), V("CIN"), V("QH0", 0, 64), ALU.subtract)
+        tt(V("RN"), V("RN"), V("QH0", 64, 128), ALU.add)
+        tt(V("GT", 0, 64), V("RN"), V("HB"), ALU.mult)
+        ts(V("SGT", 0, 4), V("SG", 0, 4), 0.5, ALU.mult, 32.0, ALU.add)
+        for f in range(3):
+            ts(V("CLST", 8 * f, 8 * f + 8), V("SGT"), 63.0, ALU.min, 64.0 * f, ALU.add)
+        cp(V("GV"), IND(V("GT"), V("CLST")))
+        tt(V("SEL", 256, 384), V("GV", 0, 128), V("KR1"), ALU.is_equal)
+        tt(V("SEL", 0, 128), V("GV", 128, 256), V("SEL", 256, 384), ALU.mult)
+        tt(V("SEL", 128, 256), V("GV", 256, 384), V("SEL", 256, 384), ALU.mult)
+        mms([(V("QH1", 0, 384), V("BLKF"), V("SEL"))], True, True, True)
+        tt(V("MC"), V("QH1", 0, 128), V("MSK"), ALU.mult)
+        ts(V("INVF"), V("QH1", 256, 384), -512.0, ALU.mult, 512.0, ALU.add)
+        scan(V("MS"), V("SEG"), V("MC"))
+        cp(V("CHL"), V("MS", 15, 128, 16))
+        tt(V("SEND"), IND(V("U"), V("CHL")), V("INVF"), ALU.max)
+        op("G", None, [V("SEND")], [], 300, "s", t)
+
+    def grafts():
+        cp(V("KI"), V("QH1", 128, 256))
+        ts(V("IVB"), V("QH1", 256, 384), -float(BIG), ALU.mult, float(BIG), ALU.add)
+        ts(V("KEYI"), V("KI"), 10, ALU.arith_shift_right)
+        ts(V("KX"), V("KEYI"), 128.0, ALU.mult)
+        tt(V("KX"), V("KX"), V("KR0"), ALU.add)
+        tt(V("KX"), V("KX"), V("IVB"), ALU.add)
+        tt(V("KM"), V("KX"), V("MSK"), ALU.mult)
+        scan(V("KMS"), V("SEG"), V("KM"))
+        kw = V("KMS", 15, 128, 16)
+        ts(V("BI", 0, 8), kw, -0.5, ALU.add)
+        tt(V("BI", 8, 16), kw, V("KC"), ALU.subtract)
+        for kc in range(8):
+            act(V("JNK"), V("KX"), ACT.Sign, V("BI", kc, kc + 1), -1.0, V("SD", kc, kc + 1))
+            e = V("EQ", 128 * kc, 128 * kc + 128)
+            ts(e, V("KX"), V("BI", 8 + kc, 9 + kc), ALU.is_lt)
+            rsum(V("SD", 8 + kc, 9 + kc), e)
+        ts(V("DLO"), V("KI"), 255, ALU.bitwise_and)
+        ts(V("DHI"), V("KI"), 8, ALU.arith_shift_right, 3, ALU.bitwise_and)
+        ts(V("DV1"), V("DHI"), -6.0, ALU.add, V("FM", 0, 1), ALU.mult)
+        ts(V("DV2"), V("DLO"), V("FM", 1, 2), ALU.mult)
+        tt(V("DV"), V("DV1"), V("DV2"), ALU.add)
+        ts(V("DVA"), V("DV"), V("FM", 2, 3), ALU.mult)
+        ts(V("DVB"), V("DV"), V("FM", 3, 4), ALU.mult)
+        ts(V("KEYW"), V("BI", 8, 16), 0.5, ALU.add, 1.0 / 128, ALU.mult)
+        ts(V("LAB", 0, 8), V("KEYW"), float(ND), ALU.is_lt)
+        ts(V("LAB", 8, 16), V("KEYW"), 2.0 * ND, ALU.is_lt)
+        tt(V("LAB", 8, 16), V("LAB", 8, 16), V("LAB", 0, 8), ALU.subtract)
+        tt(V("OF", 0, 8), V("KEYW"), V("DUM"), ALU.subtract)
+        ts(V("OF", 8, 16), V("OF", 0, 8), -float(ND), ALU.add)
+        tt(V("OF"), V("OF"), V("LAB"), ALU.mult)
+        ts(V("SD", 0, 8), V("SD", 0, 8), 0.5, ALU.mult, 64.0, ALU.add)
+        tt(V("ND1"), V("SD", 0, 8), V("SD", 8, 16), ALU.is_le)
+        for x in range(2):
+            o = V("OF", 8 * x, 8 * x + 8)
+            tt(o, o, V("ND1"), ALU.mult)
+            tt(o, o, V("DUM"), ALU.add)
+        cp(V("OFU"), V("OF"))
+        for x, (old, dv) in enumerate((("OLDA", "DVA"), ("OLDB", "DVB"))):
+            lst = V("OFU", 8 * x, 8 * x + 8)
+            ts(V(old), IND(V("INFO"), lst), V("NFM", x, x + 1), ALU.mult)
+            tt(IND(V("INFO"), lst), V(old), V(dv), ALU.add)
+
+    def receive(t):
+        R = "RECV%d" % t
+        op("R", None, [], [V(R)], 2500, "r", t)
+        lib = V("U", 128 * t, 128 * t + 128)
+        ts(V("RG"), V(R), 512.0, ALU.is_lt, 512.0, ALU.mult)
+        tt(V("RT"), lib, V("RG"), ALU.add)
+        tt(lib, V("RT"), V(R), ALU.min)
+
+    for t in range(2):
+        down()
+        donors()
+        count_send(t)
+        grafts()
+        receive(t)
+        evaluate(False, t == 1)
+    return ops
+
+
+def depend(ops):
+    hist = {}
+    for n, o in enumerate(ops):
+        dep = set()
+        for wr, vs in ((False, o["rd"]), (True, o["wr"])):
+            for v in vs:
+                name, a, b, s, p = v
+                ps = META[name][0] == "psum"
+                for m, mw, ma, mb, mp in hist.get(name, []):
+                    if m == n:
+                        continue
+                    if ps and ops[m]["e"] != o["e"]:
+                        if ma // 512 <= (b - 1) // 512 and a // 512 <= (mb - 1) // 512:
+                            dep.add(m)
+                        continue
+                    if not (wr or mw) or ma >= b or a >= mb:
+                        continue
+                    if p is not None and mp is not None and p[2] == 16 and mp[2] == 16 and p[0] != mp[0]:
+                        continue
+                    dep.add(m)
+        for wr, vs in ((False, o["rd"]), (True, o["wr"])):
+            for name, a, b, s, p in vs:
+                h = hist.setdefault(name, [])
+                if wr and s == 1 and p is None and META[name][0] != "psum":
+                    h[:] = [x for x in h if not (a <= x[2] and x[3] <= b and x[0] != n)]
+                h.append((n, wr, a, b, p))
+        o["dep"] = dep
+        if o["k"] == "r":
+            o["dep"] = {m for m in range(n) if ops[m]["k"] == "s" and ops[m]["i"] == o["i"]}
+
+
+def schedule(ops):
+    N = len(ops)
+    succ = [[] for _ in range(N)]
+    for n, o in enumerate(ops):
+        for m in o["dep"]:
+            succ[m].append(n)
+    prio = [0.0] * N
+    for n in range(N - 1, -1, -1):
+        prio[n] = ops[n]["c"] + 60 + max([prio[m] for m in succ[n]] + [0.0])
+    prio = [x + o["b"] for x, o in zip(prio, ops)]
+    left = [len(o["dep"]) for o in ops]
+    fin = [0.0] * N
+    free, rdy = {}, {}
+    for n, o in enumerate(ops):
+        if left[n] == 0:
+            rdy.setdefault(o["e"], {})[n] = 0.0
+    order = []
+    while len(order) < N:
+        best = None
+        for e in rdy:
+            if not rdy[e]:
+                continue
+            f = free.get(e, 0.0)
+            t0 = min(max(f, t) for t in rdy[e].values())
+            c = max((n for n, t in rdy[e].items() if max(f, t) <= t0 + 40), key=lambda n: (prio[n], -n))
+            st = max(f, rdy[e][c])
+            if best is None or (st, e) < best[:2]:
+                best = (st, e, c)
+        st, e, n = best
+        del rdy[e][n]
+        o = ops[n]
+        fin[n] = st + o["c"]
+        free[e] = st + 80 if o["k"] == "d" else st if o["k"] == "r" else fin[n]
+        order.append(n)
+        for m in succ[n]:
+            left[m] -= 1
+            if left[m] == 0:
+                q = ops[m]["e"]
+                rdy.setdefault(q, {})[m] = max(fin[d] + (60 if ops[d]["e"] == q else 100) for d in ops[m]["dep"])
+    return order, fin
+
+
+_CACHE = {}
+
+
+def plan():
+    if not _CACHE:
+        ops = build()
+        depend(ops)
+        order, fin = schedule(ops)
+        _CACHE["ops"], _CACHE["order"], _CACHE["fin"] = ops, order, fin
+    return _CACHE
+
+
+def rank_program(g, core, T, topo):
+    rank = T.rank_of(core)
+    if rank is None:
+        return
+    pl = plan()
+    ops, order = pl["ops"], pl["order"]
+    dst = T.cores[(rank + 1) % len(T.cores)]
+    rid, pid = topo.addr(dst)[:2]
+    eng = topo.engines(core, dst)[:8]
+    mask = sum(1 << e for e in eng)
+    queue = {"V": g.vector, "A": g.scalar, "T": g.tensor, "G": g, "S": g.sync}
+    csem = {"V": "sV", "A": "sA", "T": "sT", "G": "sG"}
+    count = {}
+    known = {}
+    done = {}
+    clock = {}
+    nd = [0]
+    for n in order:
+        o = ops[n]
+        k = o["k"]
+        if k == "r":
+            done[n] = ("rs%d" % o["i"], len(eng))
+            count[done[n][0]] = len(eng)
+            clock[n] = {done[n][0]: len(eng)}
+            continue
+        q = queue[o["e"]]
+        kn = known.setdefault(o["e"], {})
+        need = {}
+        for d in o["dep"]:
+            s, c = done[d]
+            if need.get(s, (0, 0))[0] < c:
+                need[s] = (c, d)
+        for s, (c, d) in sorted(need.items(), key=lambda x: -x[1][1]):
+            if kn.get(s, 0) >= c:
+                continue
+            q.wait_ge(T.sem[s], c)
+            for s2, c2 in clock[d].items():
+                if kn.get(s2, 0) < c2:
+                    kn[s2] = c2
+        if k == "s":
+            s = "ls%d" % o["i"]
+            g.remote_dma(T["RECV%d" % o["i"]][:], T["SEND"][:], T.sem["rs%d" % o["i"]], T.sem[s], pid, rid, mask)
+            done[n] = (s, len(eng))
+        elif k == "d":
+            s = "d%d" % nd[0]
+            nd[0] += 1
+            o["f"](g, T).then_inc(T.sem[s], 16)
+            done[n] = (s, 16)
+        else:
+            s = csem[o["e"]]
+            o["f"](g, T).then_inc(T.sem[s], 1)
+            done[n] = (s, count.get(s, 0) + 1)
+        count[s] = done[n][1]
+        clock[n] = dict(kn)
+        clock[n][s] = count[s]
+    for s in sorted(count):
+        g.wait_ge(T.sem[s], count[s])

@@ -2,10 +2,11 @@ from concourse.mybir import AluOpType, ActivationFunctionType, AxisListType
 
 ALU = AluOpType
 ACT = ActivationFunctionType
-X = AxisListType.X
 FX, GC, PC = 15.0, 1.3, 0.42
 HB0 = 2000.0
-CH = ((0, 256, "V"), (256, 256, "A"), (512, 256, "V"), (768, 256, "V"))
+KS = (1,)
+CH = ((0, 256, "V"), (256, 256, "V"), (512, 256, "V"), (768, 128, "A"), (896, 128, "A"))
+BANKS = (("QH0", 0), ("QH0", 512), ("QH1", 0), ("QH1", 512), ("ZZ", 512))
 L, A0, ND, W = 1024, 1536, 4096, 5632
 BIG = 1 << 20
 
@@ -29,21 +30,21 @@ def _halves(text):
     return " ".join(n.replace(":", h + ":") for h in "01" for n in text.split())
 
 
-_bufs("U:5632 AT:4096 BT:4096 INFO:4224 SALL:2048 WA:2048 WB:2048 C1:2048 C2:2048 WBA:2048 N5B:128 P5B:128 IDB:128 NIB:128 BLK:128 LTI:128 "
+_bufs("U:5632 AT:4096 BT:4096 INFO:4224 SALL:2048 WA:2048 WB:2048 S4K:2048 C1:2048 C2:2048 WBA:2048 N5B:128 P5B:128 IDB:128 NIB:128 BLK:128 LTI:128 "
       "T4:128 LV:1536 TG:1024 TGC:1024 KH:512 KLO:512 YO:5632 YT:4096 WTB:2 HB:64 INVF:128 SEND:128 RECV0:128 RECV1:128 RG:128 RT:128 "
-      "DV1:128 DV2:128 DV:128 DVA:128 DVB:128 EQ:1024 OLDA:128 OLDB:128", "bfloat16")
+      "GH:64 GL:64 SLH:128 SLL:128 FM:512 DVA:128 DVB:128 OLDA:128 OLDB:128", "bfloat16")
 _bufs(_halves("WDA:1536 WDB:1536 T1:1024 ZS:1024 AB:1024 NF:512 XC:2048 AC:2048"), "bfloat16")
-_bufs(_halves("EB:32 TO:64 KAQ:64 KD:96 R:64 NDF:32 LIV:64 LQ:32 KE:64 KN:64 KDT:32 TK:32 CHD:32 CS:128 CK:128 CM:64 BST:32"))
-_bufs(_halves("UI:64 PR:32 SH:32 UA:32 STR:32 CI:128 CA:128 DI:32 DJ:32"), "int32")
+_bufs(_halves("E4:32 EB:32 KAQ:64 KD:128 R:64 NDF:32 LIV:64 KE:64 NEG:64 CS:128 CK:128 CM:64 BST:32"))
+_bufs(_halves("UI:64 PR:32 SH:32 UA:32 STR:32 CI:128 CA:128 DI:32 DJ:32 DK:32"), "int32")
 _bufs(_halves("NLA:64 NLB:64 NLC:64 CL:128"), "uint16")
 _bufs("IDF:128 BLKF:128 PF:1 PM:1 PG:1 EI:16 RA:1 RB:1 RBA:1 JQ2:32 MSK:128 RM:128 RD:128 R16:128 R8:8 SEG:128 ONE:64 KR1:128 KR0:128 KC:8 "
-      "DUM:8 JQ:64 JC:64 JT:64 MQ:128 K3F:128 WTF:2 K12:2 FM:4 NFM:2 CIN:64 RN:64 GT:192 SG:8 SGT:8 JNK:128 GV:384 SEL:384 MC:128 MS:128 "
-      "KX:128 IVB:128 KM:128 KMS:128 BI:16 SD:16 KEYW:8 ND1:8 LAB:16 OF:16 KO:512")
-_bufs("XK:512 XL:512 XH:512 WTI:2 PI:1 PJ:1 PK:1 KI:128 KEYI:128 DLO:128 DHI:128", "int32")
+      "DUM:8 JQ:64 JC:64 JT:64 MQ:128 K3F:128 WTF:2 K12:2 NFM:2 CIN:64 RN:64 GR:64 GC:64 GK:64 OH:128 SG:8 SGT:8 JNK:1024 SEL:256 MC:128 MS:128 "
+      "KX:128 KM:128 KMS:128 BI:16 SD:16 KEYW:8 ND1:8 LAB:16 OF:16 KO:512")
+_bufs("XK:512 XL:512 XH:512 WTI:2 PI:1 PJ:1 PK:1", "int32")
 _bufs("MXI:512 PI8:1 PJ8:1 PK8:1 KX0:256", "int32", rows=64)
 _bufs("NM:512 NMN:512 TE:1024 B8:128", "bfloat16", rows=64)
 _bufs("PQ8:1 PR8:1 E8:8 KXF:256", rows=64)
-_bufs("KL:512 CLST:24 CHL:8 OFU:16", "uint16")
+_bufs("KL:512 CLST:8 CHL:8 OFU:16", "uint16")
 _bufs("DH:8192 DL:8192 DN:4096", "bfloat16", "dram", 8)
 _bufs("QH0:1024 QH1:1024 SM0:512 SM1:512 ZZ:1024", "float32", "psum")
 
@@ -152,9 +153,6 @@ def build():
     def scan(out, d0, d1):
         op("V", lambda g, T: g.vector.tensor_tensor_scan(_ap(T, out), _ap(T, d0), _ap(T, d1), 0.0, ALU.mult, ALU.add), [d0, d1], [out], FX + 0.83 * _n(out))
 
-    def rsum(out, a):
-        op("V", lambda g, T: g.vector.tensor_reduce(_ap(T, out), _ap(T, a), X, ALU.add), [a], [out], FX + max(0.83 * _n(a), 53))
-
     def memset(out, c):
         op("V", lambda g, T: g.vector.memset(_ap(T, out), c), [], [out], FX + 0.42 * _n(out))
 
@@ -210,7 +208,7 @@ def build():
     for sd in range(2):
         tp(V("SM0", 64 * sd, 64 * sd + 64), V("KXF", 128 * sd, 128 * sd + 128), V("IDF", 0, 64, 1, p64))
     cp(V("KL", 0, 128), V("SM0", 0, 128))
-    bias[0] = 6000.0
+    bias[0] = 12000.0
     ts(V("PJ"), V("PI"), 15, ALU.bitwise_and)
     cp(V("PM"), V("PJ"))
     ts(V("PK"), V("PI"), 4, ALU.arith_shift_right)
@@ -233,7 +231,8 @@ def build():
     for i in range(16):
         act(V("SALL", 129 * i, 129 * i + 113, 16), V("BLK", i, 128, 16), ACT.Copy)
     bias[0] = 6000.0
-    memset(V("INFO"), 0.0)
+    for q in range(4):
+        memset(V("INFO", 1056 * q, 1056 * q + 1056), 0.0)
     ts(V("NM"), V("MXI"), -255.0, ALU.mult, 255.0, ALU.add)
     act(V("NMN"), V("NM"), ACT.Copy, 0.0, -1.0)
     ts(V("XH"), V("XK"), 8, ALU.arith_shift_right)
@@ -290,7 +289,7 @@ def build():
             win = V("U", 0, A0 + base)
             pss = []
             for q, (c0, w, eb) in enumerate(CH):
-                ps = V("QH%d" % (q // 2), 512 * (q % 2), 512 * (q % 2) + w)
+                ps = V(BANKS[q][0], BANKS[q][1], BANKS[q][1] + w)
                 pss.append(ps)
                 k0 = 2 * l + c0 // 512
                 mms([(ps, V("TE", 128 * k0, 128 * k0 + 128), V("NMN", c0 % 512, c0 % 512 + w))], True, False)
@@ -331,6 +330,7 @@ def build():
     act(V("C1"), V("SALL"), ACT.Copy, 0.0, V("WTF", 0, 1))
     act(V("C2"), V("SALL"), ACT.Copy, 0.0, V("WTF", 1, 2))
     tt(V("RBA"), V("RB"), V("RA"), ALU.subtract)
+    act(V("S4K"), V("SALL"), ACT.Copy, 0.0, 4096.0)
     act(V("WBA"), V("SALL"), ACT.Copy, 0.0, V("RBA"))
     mms([(V("SM0", 0, 2), V("BLK"), V("WTB"))])
     ts(V("K12"), V("SM0", 0, 2), 255.0, ALU.mult)
@@ -343,11 +343,12 @@ def build():
     ts(V("KR0"), V("RM"), 1.0, ALU.mult)
     ts(V("KC"), V("DUM"), V("PM"), ALU.add, 0.5, ALU.add)
     ts(V("DUM"), V("KC"), ND - 0.5, ALU.add)
-    tt(V("FM", 0, 1), V("EI", 0, 1), V("EI", 2, 3), ALU.add)
-    tt(V("FM", 1, 2), V("EI", 1, 2), V("EI", 3, 4), ALU.add)
-    tt(V("FM", 2, 3), V("EI", 0, 1), V("EI", 1, 2), ALU.add)
-    tt(V("FM", 3, 4), V("EI", 2, 3), V("EI", 3, 4), ALU.add)
-    ts(V("NFM"), V("FM", 2, 4), -1.0, ALU.mult, 1.0, ALU.add)
+    for f in range(4):
+        memset(V("FM", 128 * f, 128 * f + 128), 0.0)
+        cp(V("FM", 129 * f, 128 * f + 128, 16), V("BLK", f, 128, 16))
+    for x in range(2):
+        tt(V("NFM", x, x + 1), V("EI", 2 * x, 2 * x + 1), V("EI", 2 * x + 1, 2 * x + 2), ALU.add)
+    ts(V("NFM"), V("NFM"), -1.0, ALU.mult, 1.0, ALU.add)
 
     def down():
         for s in range(3):
@@ -358,8 +359,9 @@ def build():
                 cur, nxt = cur + H, nxt + H
                 NLn, NLp = ("NLA", "NLB", "NLC")[s] + H, ("NLA", "NLB", "NLC")[s - 1] + H
                 Q, SM, ZS, AB, NF, T1 = "QH" + H, "SM" + H, "ZS" + H, "AB" + H, "NF" + H, "T1" + H
-                R, TO, KAQ, KD, EB, KE, KN, LIV = "R" + H, "TO" + H, "KAQ" + H, "KD" + H, "EB" + H, "KE" + H, "KN" + H, "LIV" + H
+                R, KAQ, KD, EB, KE, LIV = "R" + H, "KAQ" + H, "KD" + H, "EB" + H, "KE" + H, "LIV" + H
                 jq = V("JQ", 0, 32)
+                z = 512 * h
                 bank = (V(SM), V(Q, 512, 1024))
                 if s == 0:
                     D = V("TGC", 512 * h, 512 * h + 512)
@@ -367,8 +369,9 @@ def build():
                     ka, kb = V("K3F", 32 * h, 32 * h + 32), V("K3F", 64 + 32 * h, 96 + 32 * h)
                     act(V(KAQ, 0, 32), ka, ACT.Copy)
                     act(V(KAQ, 32, 64), jq, ACT.Copy)
-                    tt(V(KD, 32, 64), kb, ka, ALU.subtract)
-                    act(V(KD, 64, 96), jq, ACT.Identity, 512.0, 0.0)
+                    tt(V(KD, 1, 64, 2), kb, ka, ALU.subtract)
+                    act(V(KD, 65, 128, 2), jq, ACT.Identity, 512.0, 0.0)
+                    act(V(KD, 64, 128, 2), V("JQ2"), ACT.Copy)
                     zs = [[(1, own[1 - x]), (-1, D)] for x in range(2)]
                     nm = (V("TE", 128 * (6 + h), 128 * (7 + h)), V("NM"))
                 else:
@@ -376,34 +379,40 @@ def build():
                     act(D, IND(V(nxt, 0, 1024 if s == 1 else 1536), V(NLp, 32, 64)), ACT.Copy)
                     nl = V(NLp, 0, 32)
                     za, yb = V(ZS, 0, 512), V(ZS, 512, 1024)
-                    act(yb, IND(V("BT", 0, 3072), nl), ACT.Copy)
+                    cp(yb, IND(V("BT", 0, 3072), nl))
                     tt(za, IND(V("AT", 0, 3072), nl), D, ALU.subtract)
                     act(V(NF), IND(V("INFO", 0, ND), nl), ACT.Copy)
                     zs = [[(1, yb), (-1, D)], [(1, za)]]
                     nm = (V("T4"), V(NF))
                 for x in range(2):
-                    q = V(Q, 512 * x, 512 * x + 512)
-                    mms([(q, V("N5B") if w > 0 else V("P5B"), r) for w, r in zs[x]])
-                    tt(V(T1, 512 * x, 512 * x + 512), q, D, ALU.max)
+                    q, t1 = V(Q, 512 * x, 512 * x + 512), V(T1, 512 * x, 512 * x + 512)
+                    if x in KS:
+                        if s == 0 or x == 0:
+                            mms([(q, V("IDB") if w > 0 else V("NIB"), r) for w, r in zs[x]])
+                        else:
+                            q = za
+                        act(t1, q, ACT.Relu, 0.0, -512.0)
+                    else:
+                        mms([(q, V("N5B") if w > 0 else V("P5B"), r) for w, r in zs[x]])
+                        tt(t1, q, D, ALU.max)
                 for x in range(2):
-                    mms([(bank[x],) + nm] + [(bank[x], V("NIB") if w > 0 else V("IDB"), r) for w, r in zs[x]])
+                    lst = [(bank[x],) + nm] + [(bank[x], V("NIB") if w > 0 else V("IDB"), r) for w, r in zs[x]]
+                    mms(lst + ([(bank[x], V("IDB"), V(T1, 512 * x, 512 * x + 512))] if x in KS else []))
                 if s > 0:
-                    z = 512 * h
-                    wrap(V("ZZ", z, z + 32), "WA", NF, 0, 512)
-                    wrap(V("ZZ", z + 32, z + 64), "WBA", NF, 0, 512)
+                    wrap(V("ZZ", z, z + 64, 2), "WA", NF, 0, 512)
+                    wrap(V("ZZ", z + 1, z + 64, 2), "WBA", NF, 0, 512)
                     ch = V(R, 0, 32)
                     act(V("NDF" + H), ch, ACT.Relu)
-                    ts(V(LIV, 0, 32), ch, 0.0, ALU.is_ge)
-                    act(V(LIV, 32, 64), V(LIV, 0, 32), ACT.Copy)
-                    act(V(KD, 64, 96), V(LIV, 0, 32), ACT.Copy, 0.0, 512.0)
-                    act(V("LQ" + H), V(LIV, 0, 32), ACT.Copy, 0.0, 1024.0)
-                    ts(V("CHD" + H), ch, 0.0, ALU.min)
-                    tt(V(KAQ, 32, 64), V("JQ2"), V("LQ" + H), ALU.subtract)
+                    ts(V(LIV, 0, 64, 2), ch, 0.0, ALU.is_ge)
+                    act(V(LIV, 1, 64, 2), V(LIV, 0, 64, 2), ACT.Copy)
+                    act(V(KD, 65, 128, 2), V(LIV, 0, 64, 2), ACT.Copy, 0.0, 512.0)
+                    act(V("NEG" + H, 32, 64), V(LIV, 0, 64, 2), ACT.Copy, 0.0, 1024.0)
+                    act(V("NEG" + H, 0, 32), ch, ACT.Relu, 0.0, -1.0)
                     tt(V(KD, 0, 64), V("ZZ", z, z + 64), V(LIV), ALU.mult)
-                    tt(V(KAQ, 0, 32), V(KD, 0, 32), V("CHD" + H), ALU.add)
+                    tt(V(KAQ), V(KD, 0, 128, 2), V("NEG" + H), ALU.subtract)
                 for x in range(2):
                     w = V(cur, 512 * x, 512 * x + 512)
-                    tt(w, bank[x], V(T1, 512 * x, 512 * x + 512), ALU.max)
+                    tt(w, bank[x], D if x in KS else V(T1, 512 * x, 512 * x + 512), ALU.max)
                     ts(w, w, 255.0, ALU.min)
                 for x in range(2):
                     q = V(Q, 512 * x, 512 * x + 512)
@@ -414,21 +423,23 @@ def build():
                     mms([(q, V("IDB"), y) for y in mine] + [(q, V("NIB"), V(cur, 512 * x, 512 * x + 512))])
                     act(V(AB, 512 * x, 512 * x + 512), q, ACT.Abs)
                 wrap(V(SM, 0, 64), "SALL", AB, 0, 1024)
-                act(V(EB), V(SM, 32, 64), ACT.Copy)
-                tt(V(TO, 0, 32), V(SM, 0, 32), V(EB), ALU.is_gt)
-                tt(V(TO, 32, 64), V(SM, 0, 32), V(EB), ALU.is_gt)
-                tt(V(KE, 32, 64) if s == 0 else V(KN, 32, 64), V(SM, 0, 32), V(EB), ALU.min)
-                tt(V(R), V(TO), V(KD, 32, 96), ALU.mult)
-                tt(V(R), V(R), V(KAQ), ALU.add)
+                cp(V(EB), V(SM, 32, 64))
+                to, r, kn = V("ZZ", z + 128, z + 192), V("ZZ", z + 192, z + 256), V("ZZ", z + 256, z + 320)
+                tt(V("ZZ", z + 128, z + 160), V(SM, 0, 32), V(EB), ALU.is_gt)
+                tt(V("ZZ", z + 160, z + 192), V(SM, 0, 32), V(EB), ALU.is_gt)
+                tt(r, to, V(KD, 1, 128, 2), ALU.mult)
+                tt(V(R), r, V(KAQ), ALU.add)
                 ts(V(NLn), V(R), 0.0, ALU.max)
-                act(V("TK" + H), V(TO, 0, 32), ACT.Copy, 0.0, float(ND))
+                kk = V("ZZ", z + 256, z + 320, 2)
+                tt(V(KE, 1, 64, 2) if s == 0 else V("ZZ", z + 257, z + 320, 2), V(SM, 0, 32), V(EB), ALU.min)
+                ts(kk, V("ZZ", z + 128, z + 160), float(ND), ALU.mult)
                 if s == 0:
-                    tt(V(KE, 0, 32), V("TK" + H), V("JT", 32 * h, 32 * h + 32), ALU.add)
+                    tt(V(KE, 0, 64, 2), kk, V("JT", 32 * h, 32 * h + 32), ALU.add)
                 else:
-                    tt(V(KN, 0, 32), V("TK" + H), V("NDF" + H), ALU.add)
-                    tt(V(KN), V(KN), V(KE), ALU.subtract)
-                    tt(V(KN), V(KN), V(LIV), ALU.mult)
-                    tt(V(KE), V(KE), V(KN), ALU.add)
+                    tt(kk, kk, V("NDF" + H), ALU.add)
+                    tt(kn, kn, V(KE), ALU.subtract)
+                    tt(kn, kn, V(LIV), ALU.mult)
+                    tt(V(KE), kn, V(KE), ALU.add)
 
     def donors():
         for h in range(2):
@@ -436,12 +447,12 @@ def build():
             bias[0] = HB0 * (1 - h)
             D = V("WDB" + H, 1024, 1536)
             act(D, IND(V("WDA" + H), V("NLC" + H, 32, 64)), ACT.Copy)
-            z = 512 * h
-            wrap(V("ZZ", z, z + 32), "C1", "WDB" + H, 1024, 1536)
-            wrap(V("ZZ", z + 32, z + 64), "C2", "WDB" + H, 1024, 1536)
+            Q = "QH" + H
+            wrap(V(Q, 512, 544), "C1", "WDB" + H, 1024, 1536)
+            wrap(V(Q, 544, 576), "C2", "WDB" + H, 1024, 1536)
             UI, CI, CA, CL, CS, CK, CM, BST = "UI" + H, "CI" + H, "CA" + H, "CL" + H, "CS" + H, "CK" + H, "CM" + H, "BST" + H
             for x in range(2):
-                ts(V(UI, 32 * x, 32 * x + 32), V("ZZ", z + 32 * x, z + 32 * x + 32), -1.0, ALU.mult, V("K12", x, x + 1), ALU.add)
+                ts(V(UI, 32 * x, 32 * x + 32), V(Q, 512 + 32 * x, 544 + 32 * x), -1.0, ALU.mult, V("K12", x, x + 1), ALU.add)
             tt(V("PR" + H), V(UI, 0, 32), V(UI, 32, 64), ALU.mult)
             ts(V("SH" + H), V("PR" + H), 5, ALU.arith_shift_right)
             ts(V("UA" + H), V(UI, 0, 32), 127, ALU.bitwise_and)
@@ -458,23 +469,25 @@ def build():
                     tt(x, win, D, ALU.subtract)
                 else:
                     act(x, win, ACT.Copy)
-                    q = V("QH" + H, 0, 512)
+                    q = V(Q, 0, 512)
                     mms([(q, V("IDB"), x), (q, V("NIB"), D)])
                     x = q
                 act(V("AC" + H, 512 * m, 512 * m + 512), x, ACT.Abs)
             tt(V(CS), V(CA), V("MQ"), ALU.add)
-            ts(V(CS), V(CS), 1.0 / 4096, ALU.mult)
-            wrap(V("SM" + H, 0, 128), "SALL", "AC" + H, 0, 2048)
+            act(V("E4" + H), V("KE" + H, 1, 64, 2), ACT.Copy, 0.0, 4096.0)
+            wrap(V("SM" + H, 0, 128), "S4K", "AC" + H, 0, 2048)
             tt(V(CK), V("SM" + H, 0, 128), V(CS), ALU.add)
             tt(V(CM), V(CK, 0, 64), V(CK, 64, 128), ALU.min)
             tt(V(BST), V(CM, 0, 32), V(CM, 32, 64), ALU.min)
-            tt(V("HB", 32 * h, 32 * h + 32), V(BST), V("KE" + H, 32, 64), ALU.is_lt)
-            ts(V("DI" + H), V(BST), 4096.0, ALU.mult)
-            ts(V("DJ" + H), V("DI" + H), 1023, ALU.bitwise_and)
-            c = 64 + 32 * h
-            act(V("GT", c, c + 32), V("R" + H, 0, 32), ACT.Identity, float(A0))
-            ts(V("KDT" + H), V("KE" + H, 0, 32), 1024.0, ALU.mult)
-            tt(V("GT", c + 64, c + 96), V("KDT" + H), V("DJ" + H), ALU.add)
+            c = 32 * h
+            tt(V("HB", c, c + 32), V(BST), V("E4" + H), ALU.is_lt)
+            cp(V("DI" + H), V(BST))
+            ts(V("DJ" + H), V("DI" + H), 255, ALU.bitwise_and)
+            ts(V("DK" + H), V("DI" + H), 8, ALU.arith_shift_right, 3, ALU.bitwise_and)
+            cp(V("GL", c, c + 32), V("DJ" + H))
+            ts(V("GH", c, c + 32), V("DK" + H), -6.0, ALU.add)
+            act(V("GC", c, c + 32), V("R" + H, 0, 32), ACT.Identity, float(A0))
+            act(V("GK", c, c + 32), V("KE" + H, 0, 64, 2), ACT.Identity, -float(BIG), 128.0)
 
     def count_send(t):
         bias[0] = 0.0
@@ -482,68 +495,52 @@ def build():
         mms([(V("QH0", 64, 128), V("LTI"), V("HB"))])
         scan(V("CIN"), V("ONE"), V("QH0", 0, 64))
         for kc in range(8):
-            if kc < 4:
-                act(V("JNK", 0, 64), V("CIN"), ACT.Sign, V("KC", kc, kc + 1), -1.0, V("SG", kc, kc + 1))
-            else:
-                e = V("EQ", 64 * kc, 64 * kc + 64)
-                ts(e, V("CIN"), V("KC", kc, kc + 1), ALU.is_lt)
-                rsum(V("SGT", kc, kc + 1), e)
-        tt(V("RN"), V("CIN"), V("QH0", 0, 64), ALU.subtract)
-        tt(V("RN"), V("RN"), V("QH0", 64, 128), ALU.add)
-        tt(V("GT", 0, 64), V("RN"), V("HB"), ALU.mult)
-        ts(V("SGT", 0, 4), V("SG", 0, 4), 0.5, ALU.mult, 32.0, ALU.add)
-        for f in range(3):
-            ts(V("CLST", 8 * f, 8 * f + 8), V("SGT"), 63.0, ALU.min, 64.0 * f, ALU.add)
-        cp(V("GV"), IND(V("GT"), V("CLST")))
-        tt(V("SEL", 256, 384), V("GV", 0, 128), V("KR1"), ALU.is_equal)
-        tt(V("SEL", 0, 128), V("GV", 128, 256), V("SEL", 256, 384), ALU.mult)
-        tt(V("SEL", 128, 256), V("GV", 256, 384), V("SEL", 256, 384), ALU.mult)
-        mms([(V("QH1", 0, 384), V("BLKF"), V("SEL"))], True, True, True)
+            act(V("JNK", 64 * kc, 64 * kc + 64), V("CIN"), ACT.Sign, V("KC", kc, kc + 1), -1.0, V("SG", kc, kc + 1))
+        tt(V("RN"), V("QH0", 0, 64), V("CIN"), ALU.subtract)
+        tt(V("RN"), V("QH0", 64, 128), V("RN"), ALU.subtract)
+        tt(V("GR"), V("RN"), V("HB"), ALU.mult)
+        ts(V("SGT"), V("SG"), 0.5, ALU.mult, 32.0, ALU.add)
+        ts(V("CLST"), V("SGT"), 63.0, ALU.min)
+        tt(V("OH"), IND(V("GR"), V("CLST")), V("KR1"), ALU.is_equal)
+        tt(V("SEL", 0, 128), IND(V("GC"), V("CLST")), V("OH"), ALU.mult)
+        tt(V("SEL", 128, 256), IND(V("GK"), V("CLST")), V("OH"), ALU.mult)
+        mms([(V("QH1", 0, 256), V("BLKF"), V("SEL"))], True, True, True)
+        tt(V("SLH"), IND(V("GH"), V("CLST")), V("OH"), ALU.mult)
+        tt(V("SLL"), IND(V("GL"), V("CLST")), V("OH"), ALU.mult)
         tt(V("MC"), V("QH1", 0, 128), V("MSK"), ALU.mult)
-        ts(V("INVF"), V("QH1", 256, 384), -512.0, ALU.mult, 512.0, ALU.add)
+        ts(V("INVF"), V("QH1", 128, 256), 0.0, ALU.is_ge, 512.0, ALU.mult)
         scan(V("MS"), V("SEG"), V("MC"))
         cp(V("CHL"), V("MS", 15, 128, 16))
         tt(V("SEND"), IND(V("U"), V("CHL")), V("INVF"), ALU.max)
         op("G", None, [V("SEND")], [], 300, "s", t)
 
     def grafts():
-        cp(V("KI"), V("QH1", 128, 256))
-        ts(V("IVB"), V("QH1", 256, 384), -float(BIG), ALU.mult, float(BIG), ALU.add)
-        ts(V("KEYI"), V("KI"), 10, ALU.arith_shift_right)
-        ts(V("KX"), V("KEYI"), 128.0, ALU.mult)
-        tt(V("KX"), V("KX"), V("KR0"), ALU.add)
-        tt(V("KX"), V("KX"), V("IVB"), ALU.add)
+        tt(V("KX"), V("QH1", 128, 256), V("KR0"), ALU.add)
         tt(V("KM"), V("KX"), V("MSK"), ALU.mult)
         scan(V("KMS"), V("SEG"), V("KM"))
         kw = V("KMS", 15, 128, 16)
         ts(V("BI", 0, 8), kw, -0.5, ALU.add)
         tt(V("BI", 8, 16), kw, V("KC"), ALU.subtract)
-        for kc in range(8):
-            act(V("JNK"), V("KX"), ACT.Sign, V("BI", kc, kc + 1), -1.0, V("SD", kc, kc + 1))
-            e = V("EQ", 128 * kc, 128 * kc + 128)
-            ts(e, V("KX"), V("BI", 8 + kc, 9 + kc), ALU.is_lt)
-            rsum(V("SD", 8 + kc, 9 + kc), e)
-        ts(V("DLO"), V("KI"), 255, ALU.bitwise_and)
-        ts(V("DHI"), V("KI"), 8, ALU.arith_shift_right, 3, ALU.bitwise_and)
-        ts(V("DV1"), V("DHI"), -6.0, ALU.add, V("FM", 0, 1), ALU.mult)
-        ts(V("DV2"), V("DLO"), V("FM", 1, 2), ALU.mult)
-        tt(V("DV"), V("DV1"), V("DV2"), ALU.add)
-        ts(V("DVA"), V("DV"), V("FM", 2, 3), ALU.mult)
-        ts(V("DVB"), V("DV"), V("FM", 3, 4), ALU.mult)
-        ts(V("KEYW"), V("BI", 8, 16), 0.5, ALU.add, 1.0 / 128, ALU.mult)
+        for kc in range(16):
+            n = 16 * (kc % 8) + 16
+            act(V("JNK", 128 * (kc % 8), 128 * (kc % 8) + n), V("KX", 0, n), ACT.Sign, V("BI", kc, kc + 1), -1.0, V("SD", kc, kc + 1))
+        for x in range(2):
+            q = V("SM1", 128 * x, 128 * x + 128)
+            mms([(q, V("FM", 256 * x, 256 * x + 128), V("SLH")), (q, V("FM", 256 * x + 128, 256 * x + 256), V("SLL"))])
+            act(V(("DVA", "DVB")[x]), q, ACT.Copy)
+        ts(V("KEYW"), V("BI", 8, 16), BIG + 0.5, ALU.add, 1.0 / 128, ALU.mult)
         ts(V("LAB", 0, 8), V("KEYW"), float(ND), ALU.is_lt)
         ts(V("LAB", 8, 16), V("KEYW"), 2.0 * ND, ALU.is_lt)
         tt(V("LAB", 8, 16), V("LAB", 8, 16), V("LAB", 0, 8), ALU.subtract)
         tt(V("OF", 0, 8), V("KEYW"), V("DUM"), ALU.subtract)
         ts(V("OF", 8, 16), V("OF", 0, 8), -float(ND), ALU.add)
         tt(V("OF"), V("OF"), V("LAB"), ALU.mult)
-        ts(V("SD", 0, 8), V("SD", 0, 8), 0.5, ALU.mult, 64.0, ALU.add)
         tt(V("ND1"), V("SD", 0, 8), V("SD", 8, 16), ALU.is_le)
         for x in range(2):
             o = V("OF", 8 * x, 8 * x + 8)
             tt(o, o, V("ND1"), ALU.mult)
             tt(o, o, V("DUM"), ALU.add)
-        cp(V("OFU"), V("OF"))
+            cp(V("OFU", 8 * x, 8 * x + 8), o)
         for x, (old, dv) in enumerate((("OLDA", "DVA"), ("OLDB", "DVB"))):
             lst = V("OFU", 8 * x, 8 * x + 8)
             ts(V(old), IND(V("INFO"), lst), V("NFM", x, x + 1), ALU.mult)

from concourse.mybir import AluOpType, ActivationFunctionType, AxisListType

ALU = AluOpType
ACT = ActivationFunctionType
FX, GC, PC = 15.0, 1.3, 0.42
HB0 = 2000.0
KS = (1,)
CH = ((0, 256, "V"), (256, 256, "V"), (512, 256, "V"), (768, 128, "A"), (896, 128, "A"))
BANKS = (("QH0", 0), ("QH0", 512), ("QH1", 0), ("QH1", 512), ("ZZ", 512))
L, A0, ND, W = 1024, 1536, 4096, 5632
BIG = 1 << 20

SCRATCH, META, PLACE = {}, {}, {}
PACK = {"float32": "PKF", "bfloat16": "PKB", "int32": "PKI", "uint16": "PKU"}


def _bufs(text, dt="float32", where="sbuf", rows=128):
    for w in text.split():
        name, cols = w.split(":")
        META[name] = (where, [rows, int(cols)], dt)
        if where == "sbuf" and rows == 128 and int(cols) <= 128 and name not in ("SEND", "RECV0", "RECV1", "WTI"):
            off = SCRATCH.get(PACK[dt], (0, (0, 0)))[1][1]
            PLACE[name] = (PACK[dt], off)
            SCRATCH[PACK[dt]] = ("sbuf", [128, off + (int(cols) + 15) // 16 * 16], dt)
        else:
            SCRATCH[name] = META[name]


def _halves(text):
    return " ".join(n.replace(":", h + ":") for h in "01" for n in text.split())


_bufs("U:5632 AT:4096 BT:4096 INFO:4224 SALL:2048 WA:2048 WB:2048 S4K:2048 C1:2048 C2:2048 WBA:2048 N5B:128 P5B:128 IDB:128 NIB:128 BLK:128 LTI:128 "
      "T4:128 LV:1536 TG:1024 TGC:1024 KH:512 KLO:512 YO:5632 YT:4096 WTB:2 HB:64 INVF:128 SEND:128 RECV0:128 RECV1:128 RG:128 RT:128 "
      "GH:64 GL:64 SLH:128 SLL:128 FM:512 DVA:128 DVB:128 OLDA:128 OLDB:128", "bfloat16")
_bufs(_halves("WDA:1536 WDB:1536 T1:1024 ZS:1024 AB:1024 NF:512 XC:2048 AC:2048"), "bfloat16")
_bufs(_halves("E4:32 EB:32 KAQ:64 KD:128 R:64 NDF:32 LIV:64 KE:64 NEG:64 CS:128 CK:128 CM:64 BST:32"))
_bufs(_halves("UI:64 PR:32 SH:32 UA:32 STR:32 CI:128 CA:128 DI:32 DJ:32 DK:32"), "int32")
_bufs(_halves("NLA:64 NLB:64 NLC:64 CL:128"), "uint16")
_bufs("IDF:128 BLKF:128 PF:1 PM:1 PG:1 EI:16 RA:1 RB:1 RBA:1 JQ2:32 MSK:128 RM:128 RD:128 R16:128 R8:8 SEG:128 ONE:64 KR1:128 KR0:128 KC:8 "
      "DUM:8 JQ:64 JC:64 JT:64 MQ:128 K3F:128 WTF:2 K12:2 NFM:2 CIN:64 RN:64 GR:64 GC:64 GK:64 OH:128 SG:8 SGT:8 JNK:1024 SEL:256 MC:128 MS:128 "
      "KX:128 KM:128 KMS:128 BI:16 SD:16 KEYW:8 ND1:8 LAB:16 OF:16 KO:512")
_bufs("XK:512 XL:512 XH:512 WTI:2 PI:1 PJ:1 PK:1", "int32")
_bufs("MXI:512 PI8:1 PJ8:1 PK8:1 KX0:256", "int32", rows=64)
_bufs("NM:512 NMN:512 TE:1024 B8:128", "bfloat16", rows=64)
_bufs("PQ8:1 PR8:1 E8:8 KXF:256", rows=64)
_bufs("KL:512 CLST:8 CHL:8 OFU:16", "uint16")
_bufs("DH:8192 DL:8192 DN:4096", "bfloat16", "dram", 8)
_bufs("QH0:1024 QH1:1024 SM0:512 SM1:512 ZZ:1024", "float32", "psum")

SEMAPHORES = ["sV", "sA", "sT", "sG", "rs0", "rs1", "ls0", "ls1"] + ["d%d" % i for i in range(60)]


def V(name, a=None, b=None, s=1, p=None):
    if a is None:
        a, b = 0, META[name][1][1]
    return (name, a, b, s, p)


def IND(win, off):
    return ("@", win, off)


def _ap(T, v):
    if isinstance(v, (int, float)):
        return v
    if v[0] == "@":
        return _ap(T, v[1]).indirect(_ap(T, v[2]))
    name, a, b, s, p = v
    name, off = PLACE.get(name, (name, 0))
    a, b, t = a + off, b + off, T[name]
    if p is None:
        return t[:, a:b] if s == 1 else t[:, a:b:s]
    if p[2] == 1:
        return t[p[0]:p[1], a:b] if s == 1 else t[p[0]:p[1], a:b:s]
    return t[p[0]:p[1]:p[2], a:b]


def _n(v):
    if v[0] == "@":
        return 16 * _n(v[2])
    return len(range(v[1], v[2], v[3]))


def _two(*vs):
    for v in vs:
        nm = v[1][0] if v[0] == "@" else v[0]
        if META[nm][2] not in ("bfloat16", "uint16"):
            return False
    return True


def _regs(vs):
    out = []
    for v in vs:
        if isinstance(v, (int, float)) or v is None:
            continue
        if v[0] == "@":
            out += [v[1], v[2]]
        else:
            out.append(v)
    return out


def build():
    ops = []
    bias = [0.0]

    def op(eng, emit, rd, wr, cost, kind="c", info=None):
        ops.append({"e": eng, "f": emit, "rd": _regs(rd) + [w[2] for w in wr if w[0] == "@"], "wr": [w[1] if w[0] == "@" else w for w in wr],
                    "c": cost, "k": kind, "i": info, "b": bias[0]})

    def vcost(out, a):
        n = _n(out)
        return 50 + GC * n if a[0] == "@" else FX + max((0.42 if _two(out, a) else 0.83) * n, 53)

    def tt(out, a, b, alu):
        n = _n(out)
        if out[0] == "@":
            c = 50 + 3.2 * n
        elif a[0] == "@":
            c = 50 + GC * n
        else:
            ps = META[a[0]][0] == "psum" or META[b[0]][0] == "psum"
            c = FX + max((0.83 if ps else 1.66) * n, 53)
        op("V", lambda g, T: g.vector.tensor_tensor(_ap(T, out), _ap(T, a), _ap(T, b), alu), [a, b], [out], c)

    def ts(out, a, s1, o0, s2=None, o1=None):
        if o1 is None:
            op("V", lambda g, T: g.vector.tensor_scalar(_ap(T, out), _ap(T, a), _ap(T, s1), None, o0), [a, s1], [out], vcost(out, a))
        else:
            op("V", lambda g, T: g.vector.tensor_scalar(_ap(T, out), _ap(T, a), _ap(T, s1), _ap(T, s2), o0, o1), [a, s1, s2], [out], vcost(out, a))

    def cp(out, a):
        op("V", lambda g, T: g.vector.tensor_copy(_ap(T, out), _ap(T, a)), [a], [out], vcost(out, a))

    def act(out, a, func, bias=0.0, scale=1.0, acc=None):
        n = _n(out)
        c = 65 + GC * n if a[0] == "@" else FX + 10 + 0.83 * max(n, 64)
        wr = [out] + ([acc] if acc is not None else [])

        def em(g, T):
            k = {}
            if not (isinstance(bias, float) and bias == 0.0):
                k["bias"] = _ap(T, bias)
            if not (isinstance(scale, float) and scale == 1.0):
                k["scale"] = _ap(T, scale)
            if acc is not None:
                k["accum_out"] = _ap(T, acc)
            return g.scalar.activation(_ap(T, out), _ap(T, a), func, **k)
        op("A", em, [a, bias, scale], wr, c)

    def scan(out, d0, d1):
        op("V", lambda g, T: g.vector.tensor_tensor_scan(_ap(T, out), _ap(T, d0), _ap(T, d1), 0.0, ALU.mult, ALU.add), [d0, d1], [out], FX + 0.83 * _n(out))

    def memset(out, c):
        op("V", lambda g, T: g.vector.memset(_ap(T, out), c), [], [out], FX + 0.42 * _n(out))

    def iota(out, pattern, base, cm, flag=True):
        if flag:
            op("G", lambda g, T: g.iota(_ap(T, out), pattern, base, cm, allow_small_or_imprecise_dtypes=True), [], [out], 130 + 1.66 * _n(out))
        else:
            op("G", lambda g, T: g.iota(_ap(T, out), pattern, base, cm), [], [out], 130 + 1.66 * _n(out))

    def mms(lst, start=True, stop=True, f32=False):
        c = 40.0
        for o, w, r in lst:
            c += PC * max(64, _n(r)) * (4 if f32 else 1)

        def em(g, T):
            last = None
            for q, (o, w, r) in enumerate(lst):
                last = g.tensor.matmul(_ap(T, o), _ap(T, w), _ap(T, r), start and q == 0, stop and q == len(lst) - 1)
            return last
        op("T", em, [w for o, w, r in lst] + [r for o, w, r in lst] + ([] if start else [lst[0][0]]), [lst[0][0]], c)

    def tp(out, a, ident):
        op("T", lambda g, T: g.tensor.transpose(_ap(T, out), _ap(T, a), _ap(T, ident)), [a, ident], [out], 200)

    def dma(q, out, a, c=2000):
        def em(g, T):
            return {"S": g.sync, "A": g.scalar}[q].dma_start(_ap(T, out), _ap(T, a))
        op(q, em, [a] if a[0] in META else [], [out] if out[0] in META else [], c, "d")

    def wrap(out, mats, src, a, b):
        mms([(out, V(mats, 128 * i, 128 * i + 128), V(src, a + i, b, 16)) for i in range(16)])

    dma("S", V("LV"), ("lv", 0, A0, 1, None), 2500)
    for gq in range(8):
        for sd in range(2):
            dma("S" if gq < 4 else "A", V("KX0", sd * 128 + gq * 16, sd * 128 + gq * 16 + 16), ("kid", sd * ND, sd * ND + 1024, 1, (gq, gq + 1, 1)), 2500)
    dma("A", V("MXI"), ("mx", 0, ND, 1, None))
    dma("S", V("XK"), ("kid", 0, 8192, 1, None))
    dma("S", V("TG"), ("tg", 0, 1024, 1, None))
    dma("S", V("WTI"), ("wt", 0, 2, 1, None))
    bias[0] = 20000.0
    iota(V("PI"), [[0, 1]], 0, 1, False)
    iota(V("RM"), [[1, 128]], 0, 0)
    iota(V("RD"), [[1, 8], [0, 16]], 0, 0)
    iota(V("PI8"), [[0, 1]], 0, 1, False)
    iota(V("R16"), [[0, 8], [1, 16]], 0, 0)
    iota(V("R8"), [[1, 8]], 0, 0)
    cp(V("PF"), V("PI"))
    ts(V("IDF"), V("RM"), V("PF"), ALU.is_equal)
    cp(V("KXF"), V("KX0"))
    act(V("U", 0, A0), V("LV"), ACT.Identity, 255.0, -1.0)
    p64 = (0, 64, 1)
    for sd in range(2):
        tp(V("SM0", 64 * sd, 64 * sd + 64), V("KXF", 128 * sd, 128 * sd + 128), V("IDF", 0, 64, 1, p64))
    cp(V("KL", 0, 128), V("SM0", 0, 128))
    bias[0] = 12000.0
    ts(V("PJ"), V("PI"), 15, ALU.bitwise_and)
    cp(V("PM"), V("PJ"))
    ts(V("PK"), V("PI"), 4, ALU.arith_shift_right)
    cp(V("PG"), V("PK"))
    ts(V("BLK"), V("RD"), V("PG"), ALU.is_equal)
    ts(V("EI"), V("R16", 0, 16), V("PM"), ALU.is_equal)
    ts(V("RA"), V("EI", 0, 1), 256.0, ALU.mult, V("EI", 1, 2), ALU.add)
    ts(V("RB"), V("EI", 2, 3), 256.0, ALU.mult, V("EI", 3, 4), ALU.add)
    cp(V("IDB"), V("IDF"))
    ts(V("PJ8"), V("PI8"), 7, ALU.bitwise_and)
    cp(V("PR8"), V("PJ8"))
    ts(V("PK8"), V("PI8"), 3, ALU.arith_shift_right)
    cp(V("PQ8"), V("PK8"))
    ts(V("B8"), V("RD", 0, 128, 1, p64), V("PQ8"), ALU.is_equal)
    ts(V("E8"), V("R8", 0, 8, 1, p64), V("PR8"), ALU.is_equal)
    for q in range(8):
        act(V("TE", 128 * q, 128 * q + 128), V("B8"), ACT.Copy, 0.0, V("E8", q, q + 1))
    bias[0] = 3000.0
    memset(V("SALL"), 0.0)
    for i in range(16):
        act(V("SALL", 129 * i, 129 * i + 113, 16), V("BLK", i, 128, 16), ACT.Copy)
    bias[0] = 6000.0
    for q in range(4):
        memset(V("INFO", 1056 * q, 1056 * q + 1056), 0.0)
    ts(V("NM"), V("MXI"), -255.0, ALU.mult, 255.0, ALU.add)
    act(V("NMN"), V("NM"), ACT.Copy, 0.0, -1.0)
    ts(V("XH"), V("XK"), 8, ALU.arith_shift_right)
    ts(V("XL"), V("XK"), 255, ALU.bitwise_and)
    ts(V("KH"), V("XH"), -6.0, ALU.add)
    cp(V("KLO"), V("XL"))
    dma("S", V("DH"), V("KH"))
    dma("S", V("DL"), V("KLO"))
    dma("S", V("DN"), V("NM"))
    for f, (d, a) in enumerate((("DH", 0), ("DL", 0), ("DH", ND), ("DL", ND), ("DN", 0))):
        dma("S", V("INFO", 0, ND, 1, (f, 128, 16)), V(d, a, a + ND))
    bias[0] = 2000.0
    ts(V("WA"), V("SALL"), V("RA"), ALU.mult)
    ts(V("WB"), V("SALL"), V("RB"), ALU.mult)
    bias[0] = 0.0

    def relist(l):
        P = ("SM0", "SM1")[l & 1]
        wrap(V(P, 0, 64), "WA", "INFO", 1024 * l, 1024 * l + 1024)
        wrap(V(P, 64, 128), "WB", "INFO", 1024 * l, 1024 * l + 1024)
        ts(V("KL", 128 * l, 128 * l + 128), V(P, 0, 128), float(A0), ALU.add)
        if l == 3:
            act(V("K3F"), V(P, 0, 128), ACT.Copy)

    def outputs(l):
        if l == 0:
            ts(V("YO", 0, A0), V("U", 0, A0), -1.0, ALU.mult, 255.0, ALU.add)
            dma("S", ("yo", 0, A0, 1, None), V("YO", 0, A0))
        for c0 in (1024 * l, 1024 * l + 512):
            u, yt, yo = V("U", A0 + c0, A0 + c0 + 512), V("YT", c0, c0 + 512), V("YO", A0 + c0, A0 + c0 + 512)
            if l < 3:
                act(yt, u, ACT.Relu)
                act(yo, yt, ACT.Identity, 255.0, -1.0)
            else:
                ts(yt, u, -1.0, ALU.mult, 0.0, ALU.min)
                ts(yo, yt, 255.0, ALU.add)
            dma("S", ("yo", A0 + c0, A0 + c0 + 512, 1, None), yo)
        if l == 0:
            lst = []
            for q in range(8):
                rhs = V("INFO", 512 * q, 512 * q + 512)
                lst.append((V("ZZ", 0, 512), V("WA", 128 * q, 128 * q + 128), rhs))
                lst.append((V("ZZ", 0, 512), V("WB", 128 * (8 + q), 128 * (8 + q) + 128), rhs))
            for q in range(0, 16, 2):
                mms(lst[q:q + 2], q == 0, q == 14)
            act(V("KO"), V("ZZ", 0, 512), ACT.Identity, float(A0))
            dma("S", ("ko", 0, 8192, 1, None), V("KO"))

    def evaluate(first, final):
        if not first:
            relist(0)
        for l in range(4):
            base = 1024 * l
            win = V("U", 0, A0 + base)
            pss = []
            for q, (c0, w, eb) in enumerate(CH):
                ps = V(BANKS[q][0], BANKS[q][1], BANKS[q][1] + w)
                pss.append(ps)
                k0 = 2 * l + c0 // 512
                mms([(ps, V("TE", 128 * k0, 128 * k0 + 128), V("NMN", c0 % 512, c0 % 512 + w))], True, False)
            for q, (c0, w, eb) in enumerate(CH):
                c, k0 = base + c0, 128 * l + c0 // 16
                act(V("AT", c, c + w), IND(win, V("KL", k0, k0 + w // 16)), ACT.Relu)
                off = V("KL", k0 + 64, k0 + 64 + w // 16)
                if eb == "A":
                    act(V("BT", c, c + w), IND(win, off), ACT.Relu)
                else:
                    ts(V("BT", c, c + w), IND(win, off), 0.0, ALU.max)
            for q, (c0, w, eb) in enumerate(CH):
                c, ps = base + c0, pss[q]
                mms([(ps, V("IDB"), V("AT", c, c + w)), (ps, V("IDB"), V("BT", c, c + w))], False, True)
                tt(ps, ps, V("AT", c, c + w), ALU.min)
                tt(V("U", A0 + c, A0 + c + w), ps, V("BT", c, c + w), ALU.min)
            if l < 3:
                relist(l + 1)
            if final:
                outputs(l)

    evaluate(True, False)

    ts(V("NIB"), V("IDB"), -1.0, ALU.mult)
    ts(V("N5B"), V("IDB"), -512.0, ALU.mult)
    ts(V("P5B"), V("IDB"), 512.0, ALU.mult)
    ts(V("TGC"), V("TG"), -1.0, ALU.mult, 255.0, ALU.add)
    ts(V("T4"), V("BLK"), V("EI", 4, 5), ALU.mult)
    iota(V("JC"), [[16, 64]], 0, 0)
    iota(V("KR1"), [[1, 128]], 1, 0)
    iota(V("MQ"), [[1024, 4], [0, 32]], 0, 0)
    iota(V("DUM"), [[16, 8]], 0, 0)
    ts(V("JQ"), V("JC"), V("PM"), ALU.add)
    ts(V("JT"), V("JQ"), 3072.0, ALU.add)
    ts(V("JQ2"), V("JQ", 0, 32), 1024.0, ALU.add)
    cp(V("WTB"), V("WTI"))
    cp(V("WTF"), V("WTI"))
    act(V("C1"), V("SALL"), ACT.Copy, 0.0, V("WTF", 0, 1))
    act(V("C2"), V("SALL"), ACT.Copy, 0.0, V("WTF", 1, 2))
    tt(V("RBA"), V("RB"), V("RA"), ALU.subtract)
    act(V("S4K"), V("SALL"), ACT.Copy, 0.0, 4096.0)
    act(V("WBA"), V("SALL"), ACT.Copy, 0.0, V("RBA"))
    mms([(V("SM0", 0, 2), V("BLK"), V("WTB"))])
    ts(V("K12"), V("SM0", 0, 2), 255.0, ALU.mult)
    ts(V("LTI"), V("RM"), V("PF"), ALU.is_ge)
    tt(V("LTI"), V("LTI"), V("BLK"), ALU.mult)
    cp(V("BLKF"), V("BLK"))
    ts(V("MSK"), V("R16"), V("PM"), ALU.is_equal)
    ts(V("SEG"), V("R16"), 0.0, ALU.is_gt)
    memset(V("ONE"), 1.0)
    ts(V("KR0"), V("RM"), 1.0, ALU.mult)
    ts(V("KC"), V("DUM"), V("PM"), ALU.add, 0.5, ALU.add)
    ts(V("DUM"), V("KC"), ND - 0.5, ALU.add)
    for f in range(4):
        memset(V("FM", 128 * f, 128 * f + 128), 0.0)
        cp(V("FM", 129 * f, 128 * f + 128, 16), V("BLK", f, 128, 16))
    for x in range(2):
        tt(V("NFM", x, x + 1), V("EI", 2 * x, 2 * x + 1), V("EI", 2 * x + 1, 2 * x + 2), ALU.add)
    ts(V("NFM"), V("NFM"), -1.0, ALU.mult, 1.0, ALU.add)

    def down():
        for s in range(3):
            for h in range(2):
                H = str(h)
                bias[0] = HB0 * (1 - h)
                cur, nxt = (("WDA", "WDB") if s % 2 == 0 else ("WDB", "WDA"))
                cur, nxt = cur + H, nxt + H
                NLn, NLp = ("NLA", "NLB", "NLC")[s] + H, ("NLA", "NLB", "NLC")[s - 1] + H
                Q, SM, ZS, AB, NF, T1 = "QH" + H, "SM" + H, "ZS" + H, "AB" + H, "NF" + H, "T1" + H
                R, KAQ, KD, EB, KE, LIV = "R" + H, "KAQ" + H, "KD" + H, "EB" + H, "KE" + H, "LIV" + H
                jq = V("JQ", 0, 32)
                z = 512 * h
                bank = (V(SM), V(Q, 512, 1024))
                if s == 0:
                    D = V("TGC", 512 * h, 512 * h + 512)
                    own = (V("AT", 3072 + 512 * h, 3584 + 512 * h), V("BT", 3072 + 512 * h, 3584 + 512 * h))
                    ka, kb = V("K3F", 32 * h, 32 * h + 32), V("K3F", 64 + 32 * h, 96 + 32 * h)
                    act(V(KAQ, 0, 32), ka, ACT.Copy)
                    act(V(KAQ, 32, 64), jq, ACT.Copy)
                    tt(V(KD, 1, 64, 2), kb, ka, ALU.subtract)
                    act(V(KD, 65, 128, 2), jq, ACT.Identity, 512.0, 0.0)
                    act(V(KD, 64, 128, 2), V("JQ2"), ACT.Copy)
                    zs = [[(1, own[1 - x]), (-1, D)] for x in range(2)]
                    nm = (V("TE", 128 * (6 + h), 128 * (7 + h)), V("NM"))
                else:
                    D = V(cur, 1024, 1536)
                    act(D, IND(V(nxt, 0, 1024 if s == 1 else 1536), V(NLp, 32, 64)), ACT.Copy)
                    nl = V(NLp, 0, 32)
                    za, yb = V(ZS, 0, 512), V(ZS, 512, 1024)
                    cp(yb, IND(V("BT", 0, 3072), nl))
                    tt(za, IND(V("AT", 0, 3072), nl), D, ALU.subtract)
                    act(V(NF), IND(V("INFO", 0, ND), nl), ACT.Copy)
                    zs = [[(1, yb), (-1, D)], [(1, za)]]
                    nm = (V("T4"), V(NF))
                for x in range(2):
                    q, t1 = V(Q, 512 * x, 512 * x + 512), V(T1, 512 * x, 512 * x + 512)
                    if x in KS:
                        if s == 0 or x == 0:
                            mms([(q, V("IDB") if w > 0 else V("NIB"), r) for w, r in zs[x]])
                        else:
                            q = za
                        act(t1, q, ACT.Relu, 0.0, -512.0)
                    else:
                        mms([(q, V("N5B") if w > 0 else V("P5B"), r) for w, r in zs[x]])
                        tt(t1, q, D, ALU.max)
                for x in range(2):
                    lst = [(bank[x],) + nm] + [(bank[x], V("NIB") if w > 0 else V("IDB"), r) for w, r in zs[x]]
                    mms(lst + ([(bank[x], V("IDB"), V(T1, 512 * x, 512 * x + 512))] if x in KS else []))
                if s > 0:
                    wrap(V("ZZ", z, z + 64, 2), "WA", NF, 0, 512)
                    wrap(V("ZZ", z + 1, z + 64, 2), "WBA", NF, 0, 512)
                    ch = V(R, 0, 32)
                    act(V("NDF" + H), ch, ACT.Relu)
                    ts(V(LIV, 0, 64, 2), ch, 0.0, ALU.is_ge)
                    act(V(LIV, 1, 64, 2), V(LIV, 0, 64, 2), ACT.Copy)
                    act(V(KD, 65, 128, 2), V(LIV, 0, 64, 2), ACT.Copy, 0.0, 512.0)
                    act(V("NEG" + H, 32, 64), V(LIV, 0, 64, 2), ACT.Copy, 0.0, 1024.0)
                    act(V("NEG" + H, 0, 32), ch, ACT.Relu, 0.0, -1.0)
                    tt(V(KD, 0, 64), V("ZZ", z, z + 64), V(LIV), ALU.mult)
                    tt(V(KAQ), V(KD, 0, 128, 2), V("NEG" + H), ALU.subtract)
                for x in range(2):
                    w = V(cur, 512 * x, 512 * x + 512)
                    tt(w, bank[x], D if x in KS else V(T1, 512 * x, 512 * x + 512), ALU.max)
                    ts(w, w, 255.0, ALU.min)
                for x in range(2):
                    q = V(Q, 512 * x, 512 * x + 512)
                    if s == 0:
                        mine = [own[x]]
                    else:
                        mine = ([za, D], [yb])[x]
                    mms([(q, V("IDB"), y) for y in mine] + [(q, V("NIB"), V(cur, 512 * x, 512 * x + 512))])
                    act(V(AB, 512 * x, 512 * x + 512), q, ACT.Abs)
                wrap(V(SM, 0, 64), "SALL", AB, 0, 1024)
                cp(V(EB), V(SM, 32, 64))
                to, r, kn = V("ZZ", z + 128, z + 192), V("ZZ", z + 192, z + 256), V("ZZ", z + 256, z + 320)
                tt(V("ZZ", z + 128, z + 160), V(SM, 0, 32), V(EB), ALU.is_gt)
                tt(V("ZZ", z + 160, z + 192), V(SM, 0, 32), V(EB), ALU.is_gt)
                tt(r, to, V(KD, 1, 128, 2), ALU.mult)
                tt(V(R), r, V(KAQ), ALU.add)
                ts(V(NLn), V(R), 0.0, ALU.max)
                kk = V("ZZ", z + 256, z + 320, 2)
                tt(V(KE, 1, 64, 2) if s == 0 else V("ZZ", z + 257, z + 320, 2), V(SM, 0, 32), V(EB), ALU.min)
                ts(kk, V("ZZ", z + 128, z + 160), float(ND), ALU.mult)
                if s == 0:
                    tt(V(KE, 0, 64, 2), kk, V("JT", 32 * h, 32 * h + 32), ALU.add)
                else:
                    tt(kk, kk, V("NDF" + H), ALU.add)
                    tt(kn, kn, V(KE), ALU.subtract)
                    tt(kn, kn, V(LIV), ALU.mult)
                    tt(V(KE), kn, V(KE), ALU.add)

    def donors():
        for h in range(2):
            H = str(h)
            bias[0] = HB0 * (1 - h)
            D = V("WDB" + H, 1024, 1536)
            act(D, IND(V("WDA" + H), V("NLC" + H, 32, 64)), ACT.Copy)
            Q = "QH" + H
            wrap(V(Q, 512, 544), "C1", "WDB" + H, 1024, 1536)
            wrap(V(Q, 544, 576), "C2", "WDB" + H, 1024, 1536)
            UI, CI, CA, CL, CS, CK, CM, BST = "UI" + H, "CI" + H, "CA" + H, "CL" + H, "CS" + H, "CK" + H, "CM" + H, "BST" + H
            for x in range(2):
                ts(V(UI, 32 * x, 32 * x + 32), V(Q, 512 + 32 * x, 544 + 32 * x), -1.0, ALU.mult, V("K12", x, x + 1), ALU.add)
            tt(V("PR" + H), V(UI, 0, 32), V(UI, 32, 64), ALU.mult)
            ts(V("SH" + H), V("PR" + H), 5, ALU.arith_shift_right)
            ts(V("UA" + H), V(UI, 0, 32), 127, ALU.bitwise_and)
            ts(V("STR" + H), V("UA" + H), 2.0, ALU.mult, 1.0, ALU.add)
            tt(V(CI, 0, 32), V("SH" + H), V(UI, 32, 64), ALU.add)
            for m in range(1, 4):
                tt(V(CI, 32 * m, 32 * m + 32), V(CI, 32 * m - 32, 32 * m), V("STR" + H), ALU.add)
            ts(V(CA), V(CI), 1023, ALU.bitwise_and)
            cp(V(CL), V(CA))
            for m in range(4):
                x = V("XC" + H, 512 * m, 512 * m + 512)
                win = IND(V("U", 0, L), V(CL, 32 * m, 32 * m + 32))
                if m < 3:
                    tt(x, win, D, ALU.subtract)
                else:
                    act(x, win, ACT.Copy)
                    q = V(Q, 0, 512)
                    mms([(q, V("IDB"), x), (q, V("NIB"), D)])
                    x = q
                act(V("AC" + H, 512 * m, 512 * m + 512), x, ACT.Abs)
            tt(V(CS), V(CA), V("MQ"), ALU.add)
            act(V("E4" + H), V("KE" + H, 1, 64, 2), ACT.Copy, 0.0, 4096.0)
            wrap(V("SM" + H, 0, 128), "S4K", "AC" + H, 0, 2048)
            tt(V(CK), V("SM" + H, 0, 128), V(CS), ALU.add)
            tt(V(CM), V(CK, 0, 64), V(CK, 64, 128), ALU.min)
            tt(V(BST), V(CM, 0, 32), V(CM, 32, 64), ALU.min)
            c = 32 * h
            tt(V("HB", c, c + 32), V(BST), V("E4" + H), ALU.is_lt)
            cp(V("DI" + H), V(BST))
            ts(V("DJ" + H), V("DI" + H), 255, ALU.bitwise_and)
            ts(V("DK" + H), V("DI" + H), 8, ALU.arith_shift_right, 3, ALU.bitwise_and)
            cp(V("GL", c, c + 32), V("DJ" + H))
            ts(V("GH", c, c + 32), V("DK" + H), -6.0, ALU.add)
            act(V("GC", c, c + 32), V("R" + H, 0, 32), ACT.Identity, float(A0))
            act(V("GK", c, c + 32), V("KE" + H, 0, 64, 2), ACT.Identity, -float(BIG), 128.0)

    def count_send(t):
        bias[0] = 0.0
        mms([(V("QH0", 0, 64), V("BLK"), V("HB"))])
        mms([(V("QH0", 64, 128), V("LTI"), V("HB"))])
        scan(V("CIN"), V("ONE"), V("QH0", 0, 64))
        for kc in range(8):
            act(V("JNK", 64 * kc, 64 * kc + 64), V("CIN"), ACT.Sign, V("KC", kc, kc + 1), -1.0, V("SG", kc, kc + 1))
        tt(V("RN"), V("QH0", 0, 64), V("CIN"), ALU.subtract)
        tt(V("RN"), V("QH0", 64, 128), V("RN"), ALU.subtract)
        tt(V("GR"), V("RN"), V("HB"), ALU.mult)
        ts(V("SGT"), V("SG"), 0.5, ALU.mult, 32.0, ALU.add)
        ts(V("CLST"), V("SGT"), 63.0, ALU.min)
        tt(V("OH"), IND(V("GR"), V("CLST")), V("KR1"), ALU.is_equal)
        tt(V("SEL", 0, 128), IND(V("GC"), V("CLST")), V("OH"), ALU.mult)
        tt(V("SEL", 128, 256), IND(V("GK"), V("CLST")), V("OH"), ALU.mult)
        mms([(V("QH1", 0, 256), V("BLKF"), V("SEL"))], True, True, True)
        tt(V("SLH"), IND(V("GH"), V("CLST")), V("OH"), ALU.mult)
        tt(V("SLL"), IND(V("GL"), V("CLST")), V("OH"), ALU.mult)
        tt(V("MC"), V("QH1", 0, 128), V("MSK"), ALU.mult)
        ts(V("INVF"), V("QH1", 128, 256), 0.0, ALU.is_ge, 512.0, ALU.mult)
        scan(V("MS"), V("SEG"), V("MC"))
        cp(V("CHL"), V("MS", 15, 128, 16))
        tt(V("SEND"), IND(V("U"), V("CHL")), V("INVF"), ALU.max)
        op("G", None, [V("SEND")], [], 300, "s", t)

    def grafts():
        tt(V("KX"), V("QH1", 128, 256), V("KR0"), ALU.add)
        tt(V("KM"), V("KX"), V("MSK"), ALU.mult)
        scan(V("KMS"), V("SEG"), V("KM"))
        kw = V("KMS", 15, 128, 16)
        ts(V("BI", 0, 8), kw, -0.5, ALU.add)
        tt(V("BI", 8, 16), kw, V("KC"), ALU.subtract)
        for kc in range(16):
            n = 16 * (kc % 8) + 16
            act(V("JNK", 128 * (kc % 8), 128 * (kc % 8) + n), V("KX", 0, n), ACT.Sign, V("BI", kc, kc + 1), -1.0, V("SD", kc, kc + 1))
        for x in range(2):
            q = V("SM1", 128 * x, 128 * x + 128)
            mms([(q, V("FM", 256 * x, 256 * x + 128), V("SLH")), (q, V("FM", 256 * x + 128, 256 * x + 256), V("SLL"))])
            act(V(("DVA", "DVB")[x]), q, ACT.Copy)
        ts(V("KEYW"), V("BI", 8, 16), BIG + 0.5, ALU.add, 1.0 / 128, ALU.mult)
        ts(V("LAB", 0, 8), V("KEYW"), float(ND), ALU.is_lt)
        ts(V("LAB", 8, 16), V("KEYW"), 2.0 * ND, ALU.is_lt)
        tt(V("LAB", 8, 16), V("LAB", 8, 16), V("LAB", 0, 8), ALU.subtract)
        tt(V("OF", 0, 8), V("KEYW"), V("DUM"), ALU.subtract)
        ts(V("OF", 8, 16), V("OF", 0, 8), -float(ND), ALU.add)
        tt(V("OF"), V("OF"), V("LAB"), ALU.mult)
        tt(V("ND1"), V("SD", 0, 8), V("SD", 8, 16), ALU.is_le)
        for x in range(2):
            o = V("OF", 8 * x, 8 * x + 8)
            tt(o, o, V("ND1"), ALU.mult)
            tt(o, o, V("DUM"), ALU.add)
            cp(V("OFU", 8 * x, 8 * x + 8), o)
        for x, (old, dv) in enumerate((("OLDA", "DVA"), ("OLDB", "DVB"))):
            lst = V("OFU", 8 * x, 8 * x + 8)
            ts(V(old), IND(V("INFO"), lst), V("NFM", x, x + 1), ALU.mult)
            tt(IND(V("INFO"), lst), V(old), V(dv), ALU.add)

    def receive(t):
        R = "RECV%d" % t
        op("R", None, [], [V(R)], 2500, "r", t)
        lib = V("U", 128 * t, 128 * t + 128)
        ts(V("RG"), V(R), 512.0, ALU.is_lt, 512.0, ALU.mult)
        tt(V("RT"), lib, V("RG"), ALU.add)
        tt(lib, V("RT"), V(R), ALU.min)

    for t in range(2):
        down()
        donors()
        count_send(t)
        grafts()
        receive(t)
        evaluate(False, t == 1)
    return ops


def depend(ops):
    hist = {}
    for n, o in enumerate(ops):
        dep = set()
        for wr, vs in ((False, o["rd"]), (True, o["wr"])):
            for v in vs:
                name, a, b, s, p = v
                ps = META[name][0] == "psum"
                for m, mw, ma, mb, mp in hist.get(name, []):
                    if m == n:
                        continue
                    if ps and ops[m]["e"] != o["e"]:
                        if ma // 512 <= (b - 1) // 512 and a // 512 <= (mb - 1) // 512:
                            dep.add(m)
                        continue
                    if not (wr or mw) or ma >= b or a >= mb:
                        continue
                    if p is not None and mp is not None and p[2] == 16 and mp[2] == 16 and p[0] != mp[0]:
                        continue
                    dep.add(m)
        for wr, vs in ((False, o["rd"]), (True, o["wr"])):
            for name, a, b, s, p in vs:
                h = hist.setdefault(name, [])
                if wr and s == 1 and p is None and META[name][0] != "psum":
                    h[:] = [x for x in h if not (a <= x[2] and x[3] <= b and x[0] != n)]
                h.append((n, wr, a, b, p))
        o["dep"] = dep
        if o["k"] == "r":
            o["dep"] = {m for m in range(n) if ops[m]["k"] == "s" and ops[m]["i"] == o["i"]}


def schedule(ops):
    N = len(ops)
    succ = [[] for _ in range(N)]
    for n, o in enumerate(ops):
        for m in o["dep"]:
            succ[m].append(n)
    prio = [0.0] * N
    for n in range(N - 1, -1, -1):
        prio[n] = ops[n]["c"] + 60 + max([prio[m] for m in succ[n]] + [0.0])
    prio = [x + o["b"] for x, o in zip(prio, ops)]
    left = [len(o["dep"]) for o in ops]
    fin = [0.0] * N
    free, rdy = {}, {}
    for n, o in enumerate(ops):
        if left[n] == 0:
            rdy.setdefault(o["e"], {})[n] = 0.0
    order = []
    while len(order) < N:
        best = None
        for e in rdy:
            if not rdy[e]:
                continue
            f = free.get(e, 0.0)
            t0 = min(max(f, t) for t in rdy[e].values())
            c = max((n for n, t in rdy[e].items() if max(f, t) <= t0 + 40), key=lambda n: (prio[n], -n))
            st = max(f, rdy[e][c])
            if best is None or (st, e) < best[:2]:
                best = (st, e, c)
        st, e, n = best
        del rdy[e][n]
        o = ops[n]
        fin[n] = st + o["c"]
        free[e] = st + 80 if o["k"] == "d" else st if o["k"] == "r" else fin[n]
        order.append(n)
        for m in succ[n]:
            left[m] -= 1
            if left[m] == 0:
                q = ops[m]["e"]
                rdy.setdefault(q, {})[m] = max(fin[d] + (60 if ops[d]["e"] == q else 100) for d in ops[m]["dep"])
    return order, fin


_CACHE = {}


def plan():
    if not _CACHE:
        ops = build()
        depend(ops)
        order, fin = schedule(ops)
        _CACHE["ops"], _CACHE["order"], _CACHE["fin"] = ops, order, fin
    return _CACHE


def rank_program(g, core, T, topo):
    rank = T.rank_of(core)
    if rank is None:
        return
    pl = plan()
    ops, order = pl["ops"], pl["order"]
    dst = T.cores[(rank + 1) % len(T.cores)]
    rid, pid = topo.addr(dst)[:2]
    eng = topo.engines(core, dst)[:8]
    mask = sum(1 << e for e in eng)
    queue = {"V": g.vector, "A": g.scalar, "T": g.tensor, "G": g, "S": g.sync}
    csem = {"V": "sV", "A": "sA", "T": "sT", "G": "sG"}
    count = {}
    known = {}
    done = {}
    clock = {}
    nd = [0]
    for n in order:
        o = ops[n]
        k = o["k"]
        if k == "r":
            done[n] = ("rs%d" % o["i"], len(eng))
            count[done[n][0]] = len(eng)
            clock[n] = {done[n][0]: len(eng)}
            continue
        q = queue[o["e"]]
        kn = known.setdefault(o["e"], {})
        need = {}
        for d in o["dep"]:
            s, c = done[d]
            if need.get(s, (0, 0))[0] < c:
                need[s] = (c, d)
        for s, (c, d) in sorted(need.items(), key=lambda x: -x[1][1]):
            if kn.get(s, 0) >= c:
                continue
            q.wait_ge(T.sem[s], c)
            for s2, c2 in clock[d].items():
                if kn.get(s2, 0) < c2:
                    kn[s2] = c2
        if k == "s":
            s = "ls%d" % o["i"]
            g.remote_dma(T["RECV%d" % o["i"]][:], T["SEND"][:], T.sem["rs%d" % o["i"]], T.sem[s], pid, rid, mask)
            done[n] = (s, len(eng))
        elif k == "d":
            s = "d%d" % nd[0]
            nd[0] += 1
            o["f"](g, T).then_inc(T.sem[s], 16)
            done[n] = (s, 16)
        else:
            s = csem[o["e"]]
            o["f"](g, T).then_inc(T.sem[s], 1)
            done[n] = (s, count.get(s, 0) + 1)
        count[s] = done[n][1]
        clock[n] = dict(kn)
        clock[n][s] = count[s]
    for s in sorted(count):
        g.wait_ge(T.sem[s], count[s])
